import numpy as np
import ml_dtypes


def mxq(x, axis, fmt="e4m3"):
    dtype, down = {"e4m3": (ml_dtypes.float8_e4m3fn, 7), "e5m2": (ml_dtypes.float8_e5m2, 14)}[fmt]
    v = np.moveaxis(np.asarray(x, np.float32).astype(ml_dtypes.bfloat16).astype(np.float64), axis, -1)
    blocks = v.reshape(v.shape[:-1] + (-1, 32))
    amax = np.abs(blocks).max(-1, keepdims=True)
    byte = np.maximum(np.where(amax > 0, np.frexp(amax)[1] - 1 + 127, 0) - down, 1)
    scale = np.exp2(byte - 127.0)
    codes = (blocks / scale).astype(np.float32).astype(dtype).astype(np.float64)
    return np.moveaxis((codes * scale).reshape(v.shape), -1, axis)


WIDE = False


def mx_kscale(k):
    if not WIDE:
        return np.ones(k)
    levels = np.array([10, -10, 5, -5, 0])
    if k % 512:
        return np.exp2(np.random.permutation(np.resize(levels, k // 32))).repeat(32)
    a = np.empty((k // 512, 16))
    for p in range(k // 512):
        a[p, :8] = np.random.permutation(np.resize(levels, 8))
        for g in range(8):
            far = levels[np.abs(levels - a[p, g]) >= 10]
            a[p, g + 8] = far[np.random.randint(len(far))]
    return np.exp2(a.ravel()).repeat(32)


def f64(x):
    return np.asarray(x).astype(np.float64)


def striped(idx):
    return np.tile(np.asarray(idx).reshape(-1, 16).T, (8, 1)).astype(np.uint16)


def unstriped(offs):
    return offs[:16].T.reshape(-1).astype(np.int64)


E2M1 = np.array([0.0, 0.5, 1.0, 1.5, 2.0, 3.0, 4.0, 6.0, -0.0, -0.5, -1.0, -1.5, -2.0, -3.0, -4.0, -6.0])


def pack_weight(w, fmt):
    k, n = w.shape
    w = f64(np.asarray(w, np.float32).astype(ml_dtypes.bfloat16)).reshape(k // 32, 32, n)
    amax = np.abs(w).max(1)
    if fmt == "e4m3":
        byte = np.frexp(amax)[1] - 1 + 127 - 7
    else:
        mant, ex = np.frexp(amax / 6.0)
        byte = np.where(mant > 0.5, ex, ex - 1) + 127
    byte = np.clip(np.where(amax > 0, byte, 1), 1, 254)
    scaled = (w * np.exp2(127.0 - byte)[:, None, :]).reshape(k, n).astype(np.float32)
    by_word = np.ascontiguousarray(scaled.reshape(k // 512, 128, 4, n).transpose(0, 1, 3, 2))
    if fmt == "e4m3":
        words = by_word.astype(ml_dtypes.float8_e4m3fn).view(np.uint8)
    else:
        c = by_word.astype(ml_dtypes.float4_e2m1fn).view(np.uint8) & 0xF
        words = (c[..., 0::2] | (c[..., 1::2] << 4)).reshape(k // 512, 128, 2 * n)
    return np.ascontiguousarray(words), np.ascontiguousarray(byte.astype(np.uint8).reshape(k // 512, 16, n))


def unpack_weight(words, scales, fmt):
    g, _, n = scales.shape
    words = np.ascontiguousarray(words).reshape(g, 128, n, -1)
    if fmt == "e4m3":
        vals = words.view(ml_dtypes.float8_e4m3fn).astype(np.float64)
    else:
        nib = np.empty((g, 128, n, 4), np.uint8)
        nib[..., 0::2] = words & 0xF
        nib[..., 1::2] = words >> 4
        vals = E2M1[nib]
    vals = vals * np.repeat(np.exp2(scales.astype(np.float64) - 127.0), 8, axis=1)[..., None]
    return vals.transpose(0, 1, 3, 2).reshape(g * 512, n)


D, T, I, J, C, Q = 512, 4096, 512, 512, 1024, 128


def setup_inputs():
    n = np.random.standard_normal
    idx = np.random.permutation(T)[:I]
    fd = mx_kscale(D)
    bankp = pack_weight(n((D, T)) / fd[:, None], "e2m1")
    return {
        "query": (n((D, Q)) * 0.6 / np.sqrt(D) * fd[:, None]).astype(np.float32),
        "bank_words": bankp[0],
        "bank_scales": bankp[1],
        "bkey": (n((D, J)) / fd[:, None]).astype(np.float32),
        "tmp": (np.random.uniform(0.7, 1.3, (Q, 1))).astype(np.float32),
        "offs": striped(idx),
    }


def reference(query, bank_words, bank_scales, bkey, tmp, offs):
    idx = unstriped(offs)
    banku = unpack_weight(bank_words, bank_scales, "e2m1")
    queryq = mxq(f64(query), 0, "e4m3")
    bankidxg = banku[:, idx]
    a = queryq.T @ bankidxg
    bkeyq = mxq(f64(bkey), 0, "e4m3")
    b = queryq.T @ bkeyq
    s = np.concatenate([a, b], axis=1)
    x = s * f64(tmp)
    p = np.exp(x - np.max(x, axis=1, keepdims=True))
    y = p / np.sum(p, axis=1, keepdims=True) * 1024.0
    return y

@@ -1,0 +1,123 @@
+from contextlib import ExitStack
+
+import concourse.mybir as mybir
+
+F32 = mybir.dt.float32
+BF16 = mybir.dt.bfloat16
+I32 = mybir.dt.int32
+U32 = mybir.dt.uint32
+U16 = mybir.dt.uint16
+U8 = mybir.dt.uint8
+FP8X4 = mybir.dt.float8_e4m3fn_x4
+FP4X4 = mybir.dt.float4_e2m1fn_x4
+ALU = mybir.AluOpType
+ACT = mybir.ActivationFunctionType
+
+P = 128
+PACK = 4
+D, T, I, J, Q = 512, 4096, 512, 512, 128
+HALF = J // 2
+OUT_SCALE = 1024.0
+FLOPS = 2 * D * Q * (I + J)
+
+
+def interleave(copy, grouped, raw):
+    copy(
+        out=grouped.rearrange("p (c i) t -> p c t i", i=4),
+        in_=raw.rearrange("p t (c i) -> p c t i", i=4),
+    )
+
+
+def tile_attend_contrastprobs_kernel(tc, query, bank_words, bank_scales, bkey, tmp, offs, out):
+    nc = tc.nc
+    with ExitStack() as ctx:
+        keep = ctx.enter_context(tc.tile_pool(name="keep", bufs=1))
+        psum = ctx.enter_context(tc.psum_pool(name="psum", bufs=1))
+
+        offsets = keep.tile([P, I // 16], U16, name="offsets")
+        nc.sync.dma_start(offsets[:], offs)
+
+        spread = keep.tile([P, T], U8, name="spread", align_bytes=64)
+        nc.vector.memset(spread[:].bitcast(I32), 0)
+        nc.scalar.dma_start(out=spread[0:P:8, :].bitcast(I32), in_=bank_scales[0].bitcast(I32))
+        tmp_col = keep.tile([P, 1], F32, name="tmp_col")
+        nc.scalar.dma_start(out=tmp_col[:], in_=tmp)
+
+        q_raw = keep.tile([P, PACK, Q], F32, name="q_raw", align_bytes=64)
+        nc.sync.dma_start(out=q_raw[:], in_=query.rearrange("(p t) q -> p t q", t=PACK))
+        k_raw = keep.tile([P, PACK, J], F32, name="k_raw", align_bytes=64)
+        nc.sync.dma_start(out=k_raw[:], in_=bkey.rearrange("(p t) j -> p t j", t=PACK))
+        words = keep.tile([P, T], U16, name="words", align_bytes=64)
+        nc.sync.dma_start(out=words[:].bitcast(I32), in_=bank_words[0].bitcast(I32))
+
+        warm = keep.tile([P, 1], F32, name="warm")
+        nc.vector.memset(warm[:], 0.0)
+        warm_out = keep.tile([P, 1], F32, name="warm_out")
+        nc.scalar.activation(out=warm_out[:], in_=warm[:], func=ACT.Exp)
+
+        a_scales = keep.tile([P, I], U8, name="a_scales", align_bytes=64)
+        nc.vector.memset(a_scales[:].bitcast(I32), 0)
+
+        q_grp = keep.tile([P, Q, PACK], BF16, name="q_grp", align_bytes=64)
+        interleave(nc.vector.tensor_copy, q_grp[:], q_raw[:])
+        neg_tmp = keep.tile([P, 1], F32, name="neg_tmp")
+        nc.vector.tensor_scalar(out=neg_tmp[:], in0=tmp_col[:], scalar1=-1.0, scalar2=None, op0=ALU.mult)
+        q_codes = keep.tile([P, Q], U32, name="q_codes", align_bytes=64)
+        q_scales = keep.tile([P, Q], U8, name="q_scales", align_bytes=64)
+        nc.vector.quantize_mx(out=q_codes[:].bitcast(FP8X4), scales=q_scales[:], in_=q_grp[:].rearrange("p q t -> p (q t)"))
+
+        picked_scales = keep.tile([P, I], U8, name="picked_scales", align_bytes=64)
+        nc.vector.tensor_copy(picked_scales[:], spread[:].indirect(offsets[:]))
+        for r in range(4):
+            nc.sync.dma_start(out=a_scales[r:P:32, :].bitcast(I32), in_=picked_scales[8 * r : P : 32, :].bitcast(I32))
+
+        neg_b = keep.tile([P, J], F32, name="neg_b", align_bytes=64)
+        neg_a = keep.tile([P, I + 8], F32, name="neg_a", align_bytes=64)
+        low_b = neg_a[:, I : I + 1]
+        low_b0 = keep.tile([P, 1], F32, name="low_b0")
+        k_grp = [keep.tile([P, HALF, PACK], BF16, name=f"k_grp{h}", align_bytes=64) for h in range(2)]
+        interleave(nc.vector.tensor_copy, k_grp[0][:], k_raw[:, :, 0:HALF])
+        interleave(nc.scalar.copy, k_grp[1][:], k_raw[:, :, HALF:J])
+        banks = []
+        for h in range(2):
+            k_codes = keep.tile([P, HALF], U32, name=f"k_codes{h}", align_bytes=64)
+            k_scales = keep.tile([P, HALF], U8, name=f"k_scales{h}", align_bytes=64)
+            nc.vector.quantize_mx(out=k_codes[:].bitcast(FP8X4), scales=k_scales[:], in_=k_grp[h][:].rearrange("p j t -> p (j t)"))
+            b_sum = psum.tile([Q, HALF], F32, name=f"b_sum{h}")
+            nc.tensor.matmul_mx(out=b_sum[:], lhsT=q_codes[:].bitcast(FP8X4), lhsT_scale=q_scales[:],
+                                rhs=k_codes[:].bitcast(FP8X4), rhs_scale=k_scales[:], start=True, stop=True)
+            banks.append(b_sum)
+        nc.vector.tensor_scalar(out=neg_b[:, 0:HALF], in0=banks[0][:], scalar1=neg_tmp[:], scalar2=None,
+                                op0=ALU.mult, op1=ALU.min, accum_out=low_b0[:])
+        nc.vector.tensor_scalar(out=neg_b[:, HALF:J], in0=banks[1][:], scalar1=neg_tmp[:], scalar2=low_b0[:],
+                                op0=ALU.mult, op1=ALU.min, accum_out=low_b)
+        p_b = keep.tile([P, J], F32, name="p_b", align_bytes=64)
+        sum_b = keep.tile([P, 1], F32, name="sum_b")
+        nc.scalar.activation(out=p_b[:], in_=neg_b[:], func=ACT.Exp, scale=-1.0, bias=low_b, accum_out=sum_b[:])
+
+        picked_words = keep.tile([P, I], U16, name="picked_words", align_bytes=64)
+        nc.vector.tensor_copy(picked_words[:], words[:].indirect(offsets[:]))
+        a_sum = psum.tile([Q, I], F32, name="a_sum")
+        nc.tensor.matmul_mx(out=a_sum[:], lhsT=q_codes[:].bitcast(FP8X4), lhsT_scale=q_scales[:],
+                            rhs=picked_words[:].bitcast(FP4X4), rhs_scale=a_scales[:], start=True, stop=True)
+        sum_b_less1 = keep.tile([P, 1], F32, name="sum_b_less1")
+        nc.vector.tensor_scalar(out=sum_b_less1[:], in0=sum_b[:], scalar1=-1.0, scalar2=None, op0=ALU.add)
+        low = keep.tile([P, 1], F32, name="low")
+        nc.vector.tensor_scalar(out=neg_a[:, 0:I], in0=a_sum[:], scalar1=neg_tmp[:], scalar2=low_b,
+                                op0=ALU.mult, op1=ALU.min, accum_out=low[:])
+        p_a = keep.tile([P, I + 8], F32, name="p_a", align_bytes=64)
+        sum_a = keep.tile([P, 1], F32, name="sum_a")
+        nc.scalar.activation(out=p_a[:, 0 : I + 1], in_=neg_a[:, 0 : I + 1], func=ACT.Exp, scale=-1.0, bias=low[:], accum_out=sum_a[:])
+        shift = p_a[:, I : I + 1]
+        total = keep.tile([P, 1], F32, name="total")
+        nc.vector.tensor_scalar(out=total[:], in0=shift, scalar1=sum_b_less1[:], scalar2=sum_a[:], op0=ALU.mult, op1=ALU.add)
+        shift_k = keep.tile([P, 1], F32, name="shift_k")
+        nc.vector.tensor_scalar(out=shift_k[:], in0=shift, scalar1=OUT_SCALE, scalar2=None, op0=ALU.mult)
+        inv = keep.tile([P, 1], F32, name="inv")
+        nc.vector.reciprocal(out=inv[:], in_=total[:])
+        y_a = keep.tile([P, I], F32, name="y_a", align_bytes=64)
+        nc.vector.tensor_scalar(out=y_a[:], in0=p_a[:, 0:I], scalar1=inv[:], scalar2=OUT_SCALE, op0=ALU.mult, op1=ALU.mult)
+        nc.sync.dma_start(out=out[:, 0:I], in_=y_a[:])
+        y_b = keep.tile([P, J], F32, name="y_b", align_bytes=64)
+        nc.vector.tensor_scalar(out=y_b[:], in0=p_b[:], scalar1=inv[:], scalar2=shift_k[:], op0=ALU.mult, op1=ALU.mult)
+        nc.scalar.dma_start(out=out[:, I : I + J], in_=y_b[:])

@@ -16,7 +16,8 @@ ACT = mybir.ActivationFunctionType
 P = 128
 PACK = 4
 D, T, I, J, Q = 512, 4096, 512, 512, 128
-HALF = J // 2
+SPLIT = 336
+ROW0 = P - 16
 OUT_SCALE = 1024.0
 FLOPS = 2 * D * Q * (I + J)
 
@@ -38,8 +39,7 @@ def tile_attend_contrastprobs_kernel(tc, query, bank_words, bank_scales, bkey, t
         nc.sync.dma_start(offsets[:], offs)
 
         spread = keep.tile([P, T], U8, name="spread", align_bytes=64)
-        nc.vector.memset(spread[:].bitcast(I32), 0)
-        nc.scalar.dma_start(out=spread[0:P:8, :].bitcast(I32), in_=bank_scales[0].bitcast(I32))
+        nc.sync.dma_start(out=spread[ROW0:P, :].bitcast(I32), in_=bank_scales[0].bitcast(I32))
         tmp_col = keep.tile([P, 1], F32, name="tmp_col")
         nc.scalar.dma_start(out=tmp_col[:], in_=tmp)
 
@@ -47,7 +47,7 @@ def tile_attend_contrastprobs_kernel(tc, query, bank_words, bank_scales, bkey, t
         nc.sync.dma_start(out=q_raw[:], in_=query.rearrange("(p t) q -> p t q", t=PACK))
         k_raw = keep.tile([P, PACK, J], F32, name="k_raw", align_bytes=64)
         nc.sync.dma_start(out=k_raw[:], in_=bkey.rearrange("(p t) j -> p t j", t=PACK))
-        words = keep.tile([P, T], U16, name="words", align_bytes=64)
+        words = keep.tile([P, T], U16, name="words", tag="words", align_bytes=64)
         nc.sync.dma_start(out=words[:].bitcast(I32), in_=bank_words[0].bitcast(I32))
 
         warm = keep.tile([P, 1], F32, name="warm")
@@ -55,6 +55,7 @@ def tile_attend_contrastprobs_kernel(tc, query, bank_words, bank_scales, bkey, t
         warm_out = keep.tile([P, 1], F32, name="warm_out")
         nc.scalar.activation(out=warm_out[:], in_=warm[:], func=ACT.Exp)
 
+        nc.vector.memset(spread[0:ROW0, :].bitcast(I32), 0)
         a_scales = keep.tile([P, I], U8, name="a_scales", align_bytes=64)
         nc.vector.memset(a_scales[:].bitcast(I32), 0)
 
@@ -68,40 +69,35 @@ def tile_attend_contrastprobs_kernel(tc, query, bank_words, bank_scales, bkey, t
 
         picked_scales = keep.tile([P, I], U8, name="picked_scales", align_bytes=64)
         nc.vector.tensor_copy(picked_scales[:], spread[:].indirect(offsets[:]))
-        for r in range(4):
-            nc.sync.dma_start(out=a_scales[r:P:32, :].bitcast(I32), in_=picked_scales[8 * r : P : 32, :].bitcast(I32))
+        for g in range(4):
+            nc.scalar.dma_start(out=a_scales[32 * g : 32 * g + 4, :].bitcast(I32), in_=picked_scales[ROW0 + 4 * g : ROW0 + 4 * g + 4, :].bitcast(I32))
 
-        neg_b = keep.tile([P, J], F32, name="neg_b", align_bytes=64)
-        neg_a = keep.tile([P, I + 8], F32, name="neg_a", align_bytes=64)
-        low_b = neg_a[:, I : I + 1]
-        low_b0 = keep.tile([P, 1], F32, name="low_b0")
-        k_grp = [keep.tile([P, HALF, PACK], BF16, name=f"k_grp{h}", align_bytes=64) for h in range(2)]
-        interleave(nc.vector.tensor_copy, k_grp[0][:], k_raw[:, :, 0:HALF])
-        interleave(nc.scalar.copy, k_grp[1][:], k_raw[:, :, HALF:J])
-        banks = []
-        for h in range(2):
-            k_codes = keep.tile([P, HALF], U32, name=f"k_codes{h}", align_bytes=64)
-            k_scales = keep.tile([P, HALF], U8, name=f"k_scales{h}", align_bytes=64)
-            nc.vector.quantize_mx(out=k_codes[:].bitcast(FP8X4), scales=k_scales[:], in_=k_grp[h][:].rearrange("p j t -> p (j t)"))
-            b_sum = psum.tile([Q, HALF], F32, name=f"b_sum{h}")
-            nc.tensor.matmul_mx(out=b_sum[:], lhsT=q_codes[:].bitcast(FP8X4), lhsT_scale=q_scales[:],
-                                rhs=k_codes[:].bitcast(FP8X4), rhs_scale=k_scales[:], start=True, stop=True)
-            banks.append(b_sum)
-        nc.vector.tensor_scalar(out=neg_b[:, 0:HALF], in0=banks[0][:], scalar1=neg_tmp[:], scalar2=None,
-                                op0=ALU.mult, op1=ALU.min, accum_out=low_b0[:])
-        nc.vector.tensor_scalar(out=neg_b[:, HALF:J], in0=banks[1][:], scalar1=neg_tmp[:], scalar2=low_b0[:],
-                                op0=ALU.mult, op1=ALU.min, accum_out=low_b)
-        p_b = keep.tile([P, J], F32, name="p_b", align_bytes=64)
-        sum_b = keep.tile([P, 1], F32, name="sum_b")
-        nc.scalar.activation(out=p_b[:], in_=neg_b[:], func=ACT.Exp, scale=-1.0, bias=low_b, accum_out=sum_b[:])
+        k_grp = keep.tile([P, J, PACK], BF16, name="k_grp", align_bytes=64)
+        interleave(nc.vector.tensor_copy, k_grp[:, 0:SPLIT, :], k_raw[:, :, 0:SPLIT])
+        interleave(nc.scalar.copy, k_grp[:, SPLIT:J, :], k_raw[:, :, SPLIT:J])
+        k_codes = keep.tile([P, J], U32, name="k_codes", align_bytes=64)
+        k_scales = keep.tile([P, J], U8, name="k_scales", align_bytes=64)
+        nc.vector.quantize_mx(out=k_codes[:].bitcast(FP8X4), scales=k_scales[:], in_=k_grp[:].rearrange("p j t -> p (j t)"))
+        b_sum = psum.tile([Q, J], F32, name="b_sum")
+        nc.tensor.matmul_mx(out=b_sum[:], lhsT=q_codes[:].bitcast(FP8X4), lhsT_scale=q_scales[:],
+                            rhs=k_codes[:].bitcast(FP8X4), rhs_scale=k_scales[:], start=True, stop=True)
 
         picked_words = keep.tile([P, I], U16, name="picked_words", align_bytes=64)
         nc.vector.tensor_copy(picked_words[:], words[:].indirect(offsets[:]))
         a_sum = psum.tile([Q, I], F32, name="a_sum")
         nc.tensor.matmul_mx(out=a_sum[:], lhsT=q_codes[:].bitcast(FP8X4), lhsT_scale=q_scales[:],
                             rhs=picked_words[:].bitcast(FP4X4), rhs_scale=a_scales[:], start=True, stop=True)
+
+        neg_a = keep.tile([P, I + 8], F32, name="neg_a", align_bytes=64)
+        low_b = neg_a[:, I : I + 1]
+        neg_b = keep.tile([P, J], F32, name="neg_b", tag="words", align_bytes=64)
+        nc.vector.tensor_scalar(out=neg_b[:], in0=b_sum[:], scalar1=neg_tmp[:], scalar2=None,
+                                op0=ALU.mult, op1=ALU.min, accum_out=low_b)
+        p_b = keep.tile([P, J], F32, name="p_b", align_bytes=64)
+        sum_b = keep.tile([P, 1], F32, name="sum_b")
+        nc.scalar.activation(out=p_b[:], in_=neg_b[:], func=ACT.Exp, scale=-1.0, bias=low_b, accum_out=sum_b[:])
         sum_b_less1 = keep.tile([P, 1], F32, name="sum_b_less1")
-        nc.vector.tensor_scalar(out=sum_b_less1[:], in0=sum_b[:], scalar1=-1.0, scalar2=None, op0=ALU.add)
+        nc.scalar.activation(out=sum_b_less1[:], in_=sum_b[:], func=ACT.Copy, bias=-1.0)
         low = keep.tile([P, 1], F32, name="low")
         nc.vector.tensor_scalar(out=neg_a[:, 0:I], in0=a_sum[:], scalar1=neg_tmp[:], scalar2=low_b,
                                 op0=ALU.mult, op1=ALU.min, accum_out=low[:])
@@ -112,7 +108,7 @@ def tile_attend_contrastprobs_kernel(tc, query, bank_words, bank_scales, bkey, t
         total = keep.tile([P, 1], F32, name="total")
         nc.vector.tensor_scalar(out=total[:], in0=shift, scalar1=sum_b_less1[:], scalar2=sum_a[:], op0=ALU.mult, op1=ALU.add)
         shift_k = keep.tile([P, 1], F32, name="shift_k")
-        nc.vector.tensor_scalar(out=shift_k[:], in0=shift, scalar1=OUT_SCALE, scalar2=None, op0=ALU.mult)
+        nc.scalar.activation(out=shift_k[:], in_=shift, func=ACT.Copy, scale=OUT_SCALE)
         inv = keep.tile([P, 1], F32, name="inv")
         nc.vector.reciprocal(out=inv[:], in_=total[:])
         y_a = keep.tile([P, I], F32, name="y_a", align_bytes=64)

@@ -16,8 +16,9 @@ ACT = mybir.ActivationFunctionType
 P = 128
 PACK = 4
 D, T, I, J, Q = 512, 4096, 512, 512, 128
-SPLIT = 336
-ROW0 = P - 16
+SPLIT = 160
+ROW0 = 32
+WORDS_AT = PACK * Q * 4
 OUT_SCALE = 1024.0
 FLOPS = 2 * D * Q * (I + J)
 
@@ -33,56 +34,56 @@ def tile_attend_contrastprobs_kernel(tc, query, bank_words, bank_scales, bkey, t
     nc = tc.nc
     with ExitStack() as ctx:
         keep = ctx.enter_context(tc.tile_pool(name="keep", bufs=1))
+        big = ctx.enter_context(tc.tile_pool(name="big", bufs=1))
         psum = ctx.enter_context(tc.psum_pool(name="psum", bufs=1))
-
-        offsets = keep.tile([P, I // 16], U16, name="offsets")
-        nc.sync.dma_start(offsets[:], offs)
-
-        spread = keep.tile([P, T], U8, name="spread", align_bytes=64)
-        nc.sync.dma_start(out=spread[ROW0:P, :].bitcast(I32), in_=bank_scales[0].bitcast(I32))
-        tmp_col = keep.tile([P, 1], F32, name="tmp_col")
-        nc.scalar.dma_start(out=tmp_col[:], in_=tmp)
-
-        q_raw = keep.tile([P, PACK, Q], F32, name="q_raw", align_bytes=64)
-        nc.sync.dma_start(out=q_raw[:], in_=query.rearrange("(p t) q -> p t q", t=PACK))
-        k_raw = keep.tile([P, PACK, J], F32, name="k_raw", align_bytes=64)
-        nc.sync.dma_start(out=k_raw[:], in_=bkey.rearrange("(p t) j -> p t j", t=PACK))
-        words = keep.tile([P, T], U16, name="words", tag="words", align_bytes=64)
-        nc.sync.dma_start(out=words[:].bitcast(I32), in_=bank_words[0].bitcast(I32))
 
         warm = keep.tile([P, 1], F32, name="warm")
         nc.vector.memset(warm[:], 0.0)
+        zeros = big.tile([P, I], U8, name="zeros", offset=WORDS_AT - I // 2)
+        nc.vector.memset(zeros[:].bitcast(I32), 0)
+        spread = keep.tile([P, T], U8, name="spread", tag="spread", align_bytes=64)
+        nc.vector.memset(spread[:].bitcast(I32), 0)
+        a_scales = keep.tile([P, I], U8, name="a_scales", align_bytes=64)
+        nc.vector.tensor_copy(out=a_scales[:].bitcast(I32), in_=zeros[:].bitcast(I32))
+        tmp_col = keep.tile([P, 1], F32, name="tmp_col")
+        nc.scalar.dma_start(out=tmp_col[:], in_=tmp)
+
+        k_raw = keep.tile([P, PACK, J], F32, name="k_raw", align_bytes=64)
+        nc.sync.dma_start(out=k_raw[:], in_=bkey.rearrange("(p t) j -> p t j", t=PACK))
+        offsets = keep.tile([P, I // 16], U16, name="offsets")
+        nc.sync.dma_start(offsets[:], offs)
+        nc.sync.dma_start(out=spread[ROW0 : ROW0 + 64 : 4, :].bitcast(I32), in_=bank_scales[0].bitcast(I32))
+        q_raw = big.tile([P, PACK, Q], F32, name="q_raw", offset=0)
+        nc.sync.dma_start(out=q_raw[:], in_=query.rearrange("(p t) q -> p t q", t=PACK))
+        words = big.tile([P, T], U16, name="words", offset=WORDS_AT)
+        nc.sync.dma_start(out=words[:].bitcast(I32), in_=bank_words[0].bitcast(I32))
+
         warm_out = keep.tile([P, 1], F32, name="warm_out")
         nc.scalar.activation(out=warm_out[:], in_=warm[:], func=ACT.Exp)
 
-        nc.vector.memset(spread[0:ROW0, :].bitcast(I32), 0)
-        a_scales = keep.tile([P, I], U8, name="a_scales", align_bytes=64)
-        nc.vector.memset(a_scales[:].bitcast(I32), 0)
-
-        q_grp = keep.tile([P, Q, PACK], BF16, name="q_grp", align_bytes=64)
-        interleave(nc.vector.tensor_copy, q_grp[:], q_raw[:])
+        grouped = keep.tile([P, J + Q, PACK], BF16, name="grouped", tag="grouped", align_bytes=64)
+        interleave(nc.vector.tensor_copy, grouped[:, 0:SPLIT, :], k_raw[:, :, 0:SPLIT])
+        interleave(nc.scalar.copy, grouped[:, SPLIT:J, :], k_raw[:, :, SPLIT:J])
         neg_tmp = keep.tile([P, 1], F32, name="neg_tmp")
         nc.vector.tensor_scalar(out=neg_tmp[:], in0=tmp_col[:], scalar1=-1.0, scalar2=None, op0=ALU.mult)
-        q_codes = keep.tile([P, Q], U32, name="q_codes", align_bytes=64)
-        q_scales = keep.tile([P, Q], U8, name="q_scales", align_bytes=64)
-        nc.vector.quantize_mx(out=q_codes[:].bitcast(FP8X4), scales=q_scales[:], in_=q_grp[:].rearrange("p q t -> p (q t)"))
 
         picked_scales = keep.tile([P, I], U8, name="picked_scales", align_bytes=64)
         nc.vector.tensor_copy(picked_scales[:], spread[:].indirect(offsets[:]))
         for g in range(4):
-            nc.scalar.dma_start(out=a_scales[32 * g : 32 * g + 4, :].bitcast(I32), in_=picked_scales[ROW0 + 4 * g : ROW0 + 4 * g + 4, :].bitcast(I32))
+            nc.scalar.dma_start(out=a_scales[32 * g : 32 * g + 4, :].bitcast(I32), in_=picked_scales[ROW0 + 16 * g : ROW0 + 16 * g + 16 : 4, :].bitcast(I32))
 
-        k_grp = keep.tile([P, J, PACK], BF16, name="k_grp", align_bytes=64)
-        interleave(nc.vector.tensor_copy, k_grp[:, 0:SPLIT, :], k_raw[:, :, 0:SPLIT])
-        interleave(nc.scalar.copy, k_grp[:, SPLIT:J, :], k_raw[:, :, SPLIT:J])
-        k_codes = keep.tile([P, J], U32, name="k_codes", align_bytes=64)
-        k_scales = keep.tile([P, J], U8, name="k_scales", align_bytes=64)
-        nc.vector.quantize_mx(out=k_codes[:].bitcast(FP8X4), scales=k_scales[:], in_=k_grp[:].rearrange("p j t -> p (j t)"))
+        interleave(nc.vector.tensor_copy, grouped[:, J : J + Q, :], q_raw[:])
+        k_codes = keep.tile([P, J], U32, name="k_codes", tag="spread", align_bytes=64)
+        k_scales = big.tile([P, J], U8, name="k_scales", offset=0, align_bytes=64)
+        nc.vector.quantize_mx(out=k_codes[:].bitcast(FP8X4), scales=k_scales[:], in_=grouped[:, 0:J, :].rearrange("p j t -> p (j t)"))
+        q_codes = keep.tile([P, Q], U32, name="q_codes", align_bytes=64)
+        q_scales = keep.tile([P, Q], U8, name="q_scales", align_bytes=64)
+        nc.vector.quantize_mx(out=q_codes[:].bitcast(FP8X4), scales=q_scales[:], in_=grouped[:, J : J + Q, :].rearrange("p q t -> p (q t)"))
         b_sum = psum.tile([Q, J], F32, name="b_sum")
         nc.tensor.matmul_mx(out=b_sum[:], lhsT=q_codes[:].bitcast(FP8X4), lhsT_scale=q_scales[:],
                             rhs=k_codes[:].bitcast(FP8X4), rhs_scale=k_scales[:], start=True, stop=True)
 
-        picked_words = keep.tile([P, I], U16, name="picked_words", align_bytes=64)
+        picked_words = keep.tile([P, I], U16, name="picked_words", tag="grouped", align_bytes=64)
         nc.vector.tensor_copy(picked_words[:], words[:].indirect(offsets[:]))
         a_sum = psum.tile([Q, I], F32, name="a_sum")
         nc.tensor.matmul_mx(out=a_sum[:], lhsT=q_codes[:].bitcast(FP8X4), lhsT_scale=q_scales[:],
@@ -90,7 +91,7 @@ def tile_attend_contrastprobs_kernel(tc, query, bank_words, bank_scales, bkey, t
 
         neg_a = keep.tile([P, I + 8], F32, name="neg_a", align_bytes=64)
         low_b = neg_a[:, I : I + 1]
-        neg_b = keep.tile([P, J], F32, name="neg_b", tag="words", align_bytes=64)
+        neg_b = big.tile([P, J], F32, name="neg_b", offset=WORDS_AT + I)
         nc.vector.tensor_scalar(out=neg_b[:], in0=b_sum[:], scalar1=neg_tmp[:], scalar2=None,
                                 op0=ALU.mult, op1=ALU.min, accum_out=low_b)
         p_b = keep.tile([P, J], F32, name="p_b", align_bytes=64)

@@ -37,8 +37,6 @@ def tile_attend_contrastprobs_kernel(tc, query, bank_words, bank_scales, bkey, t
         big = ctx.enter_context(tc.tile_pool(name="big", bufs=1))
         psum = ctx.enter_context(tc.psum_pool(name="psum", bufs=1))
 
-        warm = keep.tile([P, 1], F32, name="warm")
-        nc.vector.memset(warm[:], 0.0)
         zeros = big.tile([P, I], U8, name="zeros", offset=WORDS_AT - I // 2)
         nc.vector.memset(zeros[:].bitcast(I32), 0)
         spread = keep.tile([P, T], U8, name="spread", tag="spread", align_bytes=64)
@@ -57,9 +55,6 @@ def tile_attend_contrastprobs_kernel(tc, query, bank_words, bank_scales, bkey, t
         nc.sync.dma_start(out=q_raw[:], in_=query.rearrange("(p t) q -> p t q", t=PACK))
         words = big.tile([P, T], U16, name="words", offset=WORDS_AT)
         nc.sync.dma_start(out=words[:].bitcast(I32), in_=bank_words[0].bitcast(I32))
-
-        warm_out = keep.tile([P, 1], F32, name="warm_out")
-        nc.scalar.activation(out=warm_out[:], in_=warm[:], func=ACT.Exp)
 
         grouped = keep.tile([P, J + Q, PACK], BF16, name="grouped", tag="grouped", align_bytes=64)
         interleave(nc.vector.tensor_copy, grouped[:, 0:SPLIT, :], k_raw[:, :, 0:SPLIT])

@@ -16,9 +16,8 @@ ACT = mybir.ActivationFunctionType
 P = 128
 PACK = 4
 D, T, I, J, Q = 512, 4096, 512, 512, 128
-SPLIT = 160
+H = 256
 ROW0 = 32
-WORDS_AT = PACK * Q * 4
 OUT_SCALE = 1024.0
 FLOPS = 2 * D * Q * (I + J)
 
@@ -30,86 +29,132 @@ def interleave(copy, grouped, raw):
     )
 
 
+SPLIT0 = 64
+SPLIT2 = 88
+
+
 def tile_attend_contrastprobs_kernel(tc, query, bank_words, bank_scales, bkey, tmp, offs, out):
     nc = tc.nc
     with ExitStack() as ctx:
         keep = ctx.enter_context(tc.tile_pool(name="keep", bufs=1))
         big = ctx.enter_context(tc.tile_pool(name="big", bufs=1))
         psum = ctx.enter_context(tc.psum_pool(name="psum", bufs=1))
+        keys = bkey.rearrange("(p t) j -> p t j", t=PACK)
 
-        zeros = big.tile([P, I], U8, name="zeros", offset=WORDS_AT - I // 2)
-        nc.vector.memset(zeros[:].bitcast(I32), 0)
-        spread = keep.tile([P, T], U8, name="spread", tag="spread", align_bytes=64)
+        zeros = big.tile([P, 16384], U8, name="zeros", offset=0)
+        nc.vector.memset(zeros[:, 0:I].bitcast(I32), 0)
+        spread = keep.tile([P, T], U8, name="spread", align_bytes=64)
         nc.vector.memset(spread[:].bitcast(I32), 0)
         a_scales = keep.tile([P, I], U8, name="a_scales", align_bytes=64)
-        nc.vector.tensor_copy(out=a_scales[:].bitcast(I32), in_=zeros[:].bitcast(I32))
+        nc.vector.tensor_copy(out=a_scales[:].bitcast(I32), in_=zeros[:, 0:I].bitcast(I32))
         tmp_col = keep.tile([P, 1], F32, name="tmp_col")
         nc.scalar.dma_start(out=tmp_col[:], in_=tmp)
 
-        k_raw = keep.tile([P, PACK, J], F32, name="k_raw", align_bytes=64)
-        nc.sync.dma_start(out=k_raw[:], in_=bkey.rearrange("(p t) j -> p t j", t=PACK))
+        k0_raw = keep.tile([P, PACK, H], F32, name="k0_raw", align_bytes=64)
+        nc.sync.dma_start(out=k0_raw[:], in_=keys[:, :, 0:H])
         offsets = keep.tile([P, I // 16], U16, name="offsets")
         nc.sync.dma_start(offsets[:], offs)
         nc.sync.dma_start(out=spread[ROW0 : ROW0 + 64 : 4, :].bitcast(I32), in_=bank_scales[0].bitcast(I32))
         q_raw = big.tile([P, PACK, Q], F32, name="q_raw", offset=0)
         nc.sync.dma_start(out=q_raw[:], in_=query.rearrange("(p t) q -> p t q", t=PACK))
-        words = big.tile([P, T], U16, name="words", offset=WORDS_AT)
+        words = big.tile([P, T], U16, name="words", offset=4096)
         nc.sync.dma_start(out=words[:].bitcast(I32), in_=bank_words[0].bitcast(I32))
+        k1_raw = big.tile([P, PACK, H // 2], F32, name="k1_raw", offset=12288)
+        nc.sync.dma_start(out=k1_raw[:], in_=keys[:, :, H : H + H // 2])
 
-        grouped = keep.tile([P, J + Q, PACK], BF16, name="grouped", tag="grouped", align_bytes=64)
-        interleave(nc.vector.tensor_copy, grouped[:, 0:SPLIT, :], k_raw[:, :, 0:SPLIT])
-        interleave(nc.scalar.copy, grouped[:, SPLIT:J, :], k_raw[:, :, SPLIT:J])
+        k2_raw = big.tile([P, PACK, H // 2], F32, name="k2_raw", offset=14336)
+        nc.sync.dma_start(out=k2_raw[:], in_=keys[:, :, H + H // 2 : J])
+
+        k0_grouped = keep.tile([P, H, PACK], BF16, name="k0_grouped", align_bytes=64)
+        interleave(nc.vector.tensor_copy, k0_grouped[:, 0:SPLIT0, :], k0_raw[:, :, 0:SPLIT0])
+        interleave(nc.scalar.copy, k0_grouped[:, SPLIT0:H, :], k0_raw[:, :, SPLIT0:H])
         neg_tmp = keep.tile([P, 1], F32, name="neg_tmp")
         nc.vector.tensor_scalar(out=neg_tmp[:], in0=tmp_col[:], scalar1=-1.0, scalar2=None, op0=ALU.mult)
+        q_grouped = keep.tile([P, Q, PACK], BF16, name="q_grouped", align_bytes=64)
+        interleave(nc.scalar.copy, q_grouped[:], q_raw[:])
 
         picked_scales = keep.tile([P, I], U8, name="picked_scales", align_bytes=64)
         nc.vector.tensor_copy(picked_scales[:], spread[:].indirect(offsets[:]))
         for g in range(4):
-            nc.scalar.dma_start(out=a_scales[32 * g : 32 * g + 4, :].bitcast(I32), in_=picked_scales[ROW0 + 16 * g : ROW0 + 16 * g + 16 : 4, :].bitcast(I32))
+            nc.sync.dma_start(out=a_scales[32 * g : 32 * g + 4, :].bitcast(I32), in_=picked_scales[ROW0 + 16 * g : ROW0 + 16 * g + 16 : 4, :].bitcast(I32))
 
-        interleave(nc.vector.tensor_copy, grouped[:, J : J + Q, :], q_raw[:])
-        k_codes = keep.tile([P, J], U32, name="k_codes", tag="spread", align_bytes=64)
-        k_scales = big.tile([P, J], U8, name="k_scales", offset=0, align_bytes=64)
-        nc.vector.quantize_mx(out=k_codes[:].bitcast(FP8X4), scales=k_scales[:], in_=grouped[:, 0:J, :].rearrange("p j t -> p (j t)"))
-        q_codes = keep.tile([P, Q], U32, name="q_codes", align_bytes=64)
-        q_scales = keep.tile([P, Q], U8, name="q_scales", align_bytes=64)
-        nc.vector.quantize_mx(out=q_codes[:].bitcast(FP8X4), scales=q_scales[:], in_=grouped[:, J : J + Q, :].rearrange("p q t -> p (q t)"))
-        b_sum = psum.tile([Q, J], F32, name="b_sum")
-        nc.tensor.matmul_mx(out=b_sum[:], lhsT=q_codes[:].bitcast(FP8X4), lhsT_scale=q_scales[:],
-                            rhs=k_codes[:].bitcast(FP8X4), rhs_scale=k_scales[:], start=True, stop=True)
+        def quantize(name, grouped, n):
+            codes = keep.tile([P, n], U32, name=name + "_codes", align_bytes=64)
+            scales = keep.tile([P, n], U8, name=name + "_scales", align_bytes=64)
+            nc.vector.quantize_mx(out=codes[:].bitcast(FP8X4), scales=scales[:], in_=grouped[:].rearrange("p j t -> p (j t)"))
+            return codes, scales
 
-        picked_words = keep.tile([P, I], U16, name="picked_words", tag="grouped", align_bytes=64)
+        k0_codes, k0_scales = quantize("k0", k0_grouped, H)
+        q_codes, q_scales = quantize("q", q_grouped, Q)
+
+        def scores(acc, codes, scales):
+            nc.tensor.matmul_mx(out=acc, lhsT=q_codes[:].bitcast(FP8X4), lhsT_scale=q_scales[:],
+                                rhs=codes, rhs_scale=scales, start=True, stop=True)
+
+        bank0 = psum.tile([Q, 2 * H], F32, name="bank0")
+        bank1 = psum.tile([Q, 2 * H], F32, name="bank1")
+        b0_sum, a1_sum = bank0[:, 0:H], bank0[:, H : 2 * H]
+        a0_sum, b1_sum = bank1[:, 0:H], bank1[:, H : 2 * H]
+
+        neg_last = keep.tile([P, H + 8], F32, name="neg_last", align_bytes=64)
+        sums = keep.tile([P, 8], F32, name="sums")
+
+        def low(g):
+            return neg_last[:, H + g : H + g + 1]
+
+        def negate(g, acc, neg):
+            nc.vector.tensor_scalar(out=neg, in0=acc, scalar1=neg_tmp[:], scalar2=None if g == 0 else low(g - 1),
+                                    op0=ALU.mult, op1=ALU.min, accum_out=low(g))
+
+        def weights(g, neg, p):
+            nc.scalar.activation(out=p, in_=neg, func=ACT.Exp, scale=-1.0, bias=low(g), accum_out=sums[:, g : g + 1])
+
+        scores(b0_sum, k0_codes[:].bitcast(FP8X4), k0_scales[:])
+        neg_b0 = keep.tile([P, H], F32, name="neg_b0", align_bytes=64)
+        negate(0, b0_sum, neg_b0[:])
+        p_b0 = keep.tile([P, H], F32, name="p_b0", align_bytes=64)
+        weights(0, neg_b0[:], p_b0[:])
+
+        picked_words = keep.tile([P, I], U16, name="picked_words", align_bytes=64)
         nc.vector.tensor_copy(picked_words[:], words[:].indirect(offsets[:]))
-        a_sum = psum.tile([Q, I], F32, name="a_sum")
-        nc.tensor.matmul_mx(out=a_sum[:], lhsT=q_codes[:].bitcast(FP8X4), lhsT_scale=q_scales[:],
-                            rhs=picked_words[:].bitcast(FP4X4), rhs_scale=a_scales[:], start=True, stop=True)
+        scores(a0_sum, picked_words[:, 0:H].bitcast(FP4X4), a_scales[:, 0:H])
+        scores(a1_sum, picked_words[:, H:I].bitcast(FP4X4), a_scales[:, H:I])
 
-        neg_a = keep.tile([P, I + 8], F32, name="neg_a", align_bytes=64)
-        low_b = neg_a[:, I : I + 1]
-        neg_b = big.tile([P, J], F32, name="neg_b", offset=WORDS_AT + I)
-        nc.vector.tensor_scalar(out=neg_b[:], in0=b_sum[:], scalar1=neg_tmp[:], scalar2=None,
-                                op0=ALU.mult, op1=ALU.min, accum_out=low_b)
-        p_b = keep.tile([P, J], F32, name="p_b", align_bytes=64)
-        sum_b = keep.tile([P, 1], F32, name="sum_b")
-        nc.scalar.activation(out=p_b[:], in_=neg_b[:], func=ACT.Exp, scale=-1.0, bias=low_b, accum_out=sum_b[:])
-        sum_b_less1 = keep.tile([P, 1], F32, name="sum_b_less1")
-        nc.scalar.activation(out=sum_b_less1[:], in_=sum_b[:], func=ACT.Copy, bias=-1.0)
-        low = keep.tile([P, 1], F32, name="low")
-        nc.vector.tensor_scalar(out=neg_a[:, 0:I], in0=a_sum[:], scalar1=neg_tmp[:], scalar2=low_b,
-                                op0=ALU.mult, op1=ALU.min, accum_out=low[:])
-        p_a = keep.tile([P, I + 8], F32, name="p_a", align_bytes=64)
-        sum_a = keep.tile([P, 1], F32, name="sum_a")
-        nc.scalar.activation(out=p_a[:, 0 : I + 1], in_=neg_a[:, 0 : I + 1], func=ACT.Exp, scale=-1.0, bias=low[:], accum_out=sum_a[:])
-        shift = p_a[:, I : I + 1]
+        k1_grouped = keep.tile([P, H // 2, PACK], BF16, name="k1_grouped", align_bytes=64)
+        interleave(nc.scalar.copy, k1_grouped[:], k1_raw[:])
+        k1_codes, k1_scales = quantize("k1", k1_grouped, H // 2)
+        k2_grouped = keep.tile([P, H // 2, PACK], BF16, name="k2_grouped", align_bytes=64)
+        interleave(nc.vector.tensor_copy, k2_grouped[:, 0:SPLIT2, :], k2_raw[:, :, 0:SPLIT2])
+        interleave(nc.scalar.copy, k2_grouped[:, SPLIT2 : H // 2, :], k2_raw[:, :, SPLIT2 : H // 2])
+
+        neg_a = keep.tile([P, I], F32, name="neg_a", align_bytes=64)
+        p_a = keep.tile([P, I], F32, name="p_a", align_bytes=64)
+        negate(1, a0_sum, neg_a[:, 0:H])
+        weights(1, neg_a[:, 0:H], p_a[:, 0:H])
+        k2_codes, k2_scales = quantize("k2", k2_grouped, H // 2)
+        scores(b1_sum[:, 0 : H // 2], k1_codes[:].bitcast(FP8X4), k1_scales[:])
+        scores(b1_sum[:, H // 2 : H], k2_codes[:].bitcast(FP8X4), k2_scales[:])
+        negate(2, a1_sum, neg_a[:, H:I])
+        weights(2, neg_a[:, H:I], p_a[:, H:I])
+        negate(3, b1_sum, neg_last[:, 0:H])
+        p_last = keep.tile([P, H + 8], F32, name="p_last", align_bytes=64)
+        weights(3, neg_last[:, 0 : H + 4], p_last[:, 0 : H + 4])
+
+        terms = keep.tile([P, 4], F32, name="terms")
         total = keep.tile([P, 1], F32, name="total")
-        nc.vector.tensor_scalar(out=total[:], in0=shift, scalar1=sum_b_less1[:], scalar2=sum_a[:], op0=ALU.mult, op1=ALU.add)
-        shift_k = keep.tile([P, 1], F32, name="shift_k")
-        nc.scalar.activation(out=shift_k[:], in_=shift, func=ACT.Copy, scale=OUT_SCALE)
+        nc.vector.scalar_tensor_tensor(out=terms[:], in0=sums[:, 0:4], scalar=1.0, in1=p_last[:, H : H + 4],
+                                       op0=ALU.subtract, op1=ALU.mult, accum_out=total[:])
+        shift_k = keep.tile([P, 4], F32, name="shift_k")
+        nc.scalar.activation(out=shift_k[:], in_=p_last[:, H : H + 4], func=ACT.Copy, scale=OUT_SCALE)
         inv = keep.tile([P, 1], F32, name="inv")
         nc.vector.reciprocal(out=inv[:], in_=total[:])
-        y_a = keep.tile([P, I], F32, name="y_a", align_bytes=64)
-        nc.vector.tensor_scalar(out=y_a[:], in0=p_a[:, 0:I], scalar1=inv[:], scalar2=OUT_SCALE, op0=ALU.mult, op1=ALU.mult)
-        nc.sync.dma_start(out=out[:, 0:I], in_=y_a[:])
-        y_b = keep.tile([P, J], F32, name="y_b", align_bytes=64)
-        nc.vector.tensor_scalar(out=y_b[:], in0=p_b[:], scalar1=inv[:], scalar2=shift_k[:], op0=ALU.mult, op1=ALU.mult)
-        nc.scalar.dma_start(out=out[:, I : I + J], in_=y_b[:])
+
+        def finish(g, p, column, queue):
+            y = keep.tile([P, H], F32, name=f"y{g}", align_bytes=64)
+            nc.vector.tensor_scalar(out=y[:], in0=p, scalar1=inv[:], scalar2=shift_k[:, g : g + 1], op0=ALU.mult, op1=ALU.mult)
+            queue.dma_start(out=out[:, column : column + H], in_=y[:])
+
+        finish(0, p_b0[:], I, nc.sync)
+        finish(1, p_a[:, 0:H], 0, nc.scalar)
+        finish(2, p_a[:, H:I], H, nc.sync)
+        finish(3, p_last[:, 0:H], I + H, nc.scalar)

@@ -30,7 +30,6 @@ def interleave(copy, grouped, raw):
 
 
 SPLIT0 = 64
-SPLIT2 = 88
 
 
 def tile_attend_contrastprobs_kernel(tc, query, bank_words, bank_scales, bkey, tmp, offs, out):
@@ -73,7 +72,7 @@ def tile_attend_contrastprobs_kernel(tc, query, bank_words, bank_scales, bkey, t
         q_grouped = keep.tile([P, Q, PACK], BF16, name="q_grouped", align_bytes=64)
         interleave(nc.scalar.copy, q_grouped[:], q_raw[:])
 
-        picked_scales = keep.tile([P, I], U8, name="picked_scales", align_bytes=64)
+        picked_scales = keep.tile([P, I], U8, name="picked_scales", tag="k1_scales", align_bytes=64)
         nc.vector.tensor_copy(picked_scales[:], spread[:].indirect(offsets[:]))
         for g in range(4):
             nc.sync.dma_start(out=a_scales[32 * g : 32 * g + 4, :].bitcast(I32), in_=picked_scales[ROW0 + 16 * g : ROW0 + 16 * g + 16 : 4, :].bitcast(I32))
@@ -91,70 +90,72 @@ def tile_attend_contrastprobs_kernel(tc, query, bank_words, bank_scales, bkey, t
             nc.tensor.matmul_mx(out=acc, lhsT=q_codes[:].bitcast(FP8X4), lhsT_scale=q_scales[:],
                                 rhs=codes, rhs_scale=scales, start=True, stop=True)
 
-        bank0 = psum.tile([Q, 2 * H], F32, name="bank0")
-        bank1 = psum.tile([Q, 2 * H], F32, name="bank1")
-        b0_sum, a1_sum = bank0[:, 0:H], bank0[:, H : 2 * H]
-        a0_sum, b1_sum = bank1[:, 0:H], bank1[:, H : 2 * H]
+        b0_sum = psum.tile([Q, H], F32, name="b0_sum")
+        a0_sum = psum.tile([Q, H], F32, name="a0_sum")
+        a1_sum = psum.tile([Q, H], F32, name="a1_sum")
+        b1_sum = psum.tile([Q, H], F32, name="b1_sum")
 
-        neg_last = keep.tile([P, H + 8], F32, name="neg_last", align_bytes=64)
+        neg_last = keep.tile([P, H], F32, name="neg_last", align_bytes=64)
+        lows = keep.tile([P, 4], F32, name="lows")
         sums = keep.tile([P, 8], F32, name="sums")
 
         def low(g):
-            return neg_last[:, H + g : H + g + 1]
+            return lows[:, g : g + 1]
 
         def negate(g, acc, neg):
-            nc.vector.tensor_scalar(out=neg, in0=acc, scalar1=neg_tmp[:], scalar2=None if g == 0 else low(g - 1),
+            nc.vector.tensor_scalar(out=neg, in0=acc, scalar1=neg_tmp[:], scalar2=None,
                                     op0=ALU.mult, op1=ALU.min, accum_out=low(g))
 
         def weights(g, neg, p):
             nc.scalar.activation(out=p, in_=neg, func=ACT.Exp, scale=-1.0, bias=low(g), accum_out=sums[:, g : g + 1])
 
-        scores(b0_sum, k0_codes[:].bitcast(FP8X4), k0_scales[:])
+        scores(b0_sum[:], k0_codes[:].bitcast(FP8X4), k0_scales[:])
         neg_b0 = keep.tile([P, H], F32, name="neg_b0", align_bytes=64)
-        negate(0, b0_sum, neg_b0[:])
+        negate(0, b0_sum[:], neg_b0[:])
         p_b0 = keep.tile([P, H], F32, name="p_b0", align_bytes=64)
         weights(0, neg_b0[:], p_b0[:])
 
         picked_words = keep.tile([P, I], U16, name="picked_words", align_bytes=64)
         nc.vector.tensor_copy(picked_words[:], words[:].indirect(offsets[:]))
-        scores(a0_sum, picked_words[:, 0:H].bitcast(FP4X4), a_scales[:, 0:H])
-        scores(a1_sum, picked_words[:, H:I].bitcast(FP4X4), a_scales[:, H:I])
+        scores(a0_sum[:], picked_words[:, 0:H].bitcast(FP4X4), a_scales[:, 0:H])
+        scores(a1_sum[:], picked_words[:, H:I].bitcast(FP4X4), a_scales[:, H:I])
 
         k1_grouped = keep.tile([P, H // 2, PACK], BF16, name="k1_grouped", align_bytes=64)
         interleave(nc.scalar.copy, k1_grouped[:], k1_raw[:])
         k1_codes, k1_scales = quantize("k1", k1_grouped, H // 2)
         k2_grouped = keep.tile([P, H // 2, PACK], BF16, name="k2_grouped", align_bytes=64)
-        interleave(nc.vector.tensor_copy, k2_grouped[:, 0:SPLIT2, :], k2_raw[:, :, 0:SPLIT2])
-        interleave(nc.scalar.copy, k2_grouped[:, SPLIT2 : H // 2, :], k2_raw[:, :, SPLIT2 : H // 2])
+        interleave(nc.vector.tensor_copy, k2_grouped[:], k2_raw[:])
 
         neg_a = keep.tile([P, I], F32, name="neg_a", align_bytes=64)
         p_a = keep.tile([P, I], F32, name="p_a", align_bytes=64)
-        negate(1, a0_sum, neg_a[:, 0:H])
-        weights(1, neg_a[:, 0:H], p_a[:, 0:H])
         k2_codes, k2_scales = quantize("k2", k2_grouped, H // 2)
         scores(b1_sum[:, 0 : H // 2], k1_codes[:].bitcast(FP8X4), k1_scales[:])
         scores(b1_sum[:, H // 2 : H], k2_codes[:].bitcast(FP8X4), k2_scales[:])
-        negate(2, a1_sum, neg_a[:, H:I])
+        negate(1, a0_sum[:], neg_a[:, 0:H])
+        weights(1, neg_a[:, 0:H], p_a[:, 0:H])
+        negate(2, a1_sum[:], neg_a[:, H:I])
         weights(2, neg_a[:, H:I], p_a[:, H:I])
-        negate(3, b1_sum, neg_last[:, 0:H])
-        p_last = keep.tile([P, H + 8], F32, name="p_last", align_bytes=64)
-        weights(3, neg_last[:, 0 : H + 4], p_last[:, 0 : H + 4])
+        negate(3, b1_sum[:], neg_last[:])
+        p_last = keep.tile([P, H], F32, name="p_last", align_bytes=64)
+        weights(3, neg_last[:], p_last[:])
 
+        lowest = keep.tile([P, 1], F32, name="lowest")
+        nc.vector.tensor_reduce(out=lowest[:], in_=lows[:], axis=mybir.AxisListType.X, op=ALU.min)
+        shift_k = keep.tile([P, 4], F32, name="shift_k")
+        nc.scalar.activation(out=shift_k[:], in_=lows[:], func=ACT.Exp, scale=-1.0, bias=lowest[:])
         terms = keep.tile([P, 4], F32, name="terms")
         total = keep.tile([P, 1], F32, name="total")
-        nc.vector.scalar_tensor_tensor(out=terms[:], in0=sums[:, 0:4], scalar=1.0, in1=p_last[:, H : H + 4],
-                                       op0=ALU.subtract, op1=ALU.mult, accum_out=total[:])
-        shift_k = keep.tile([P, 4], F32, name="shift_k")
-        nc.scalar.activation(out=shift_k[:], in_=p_last[:, H : H + 4], func=ACT.Copy, scale=OUT_SCALE)
+        nc.vector.scalar_tensor_tensor(out=terms[:], in0=sums[:, 0:4], scalar=1.0 / OUT_SCALE, in1=shift_k[:],
+                                       op0=ALU.mult, op1=ALU.mult, accum_out=total[:])
         inv = keep.tile([P, 1], F32, name="inv")
         nc.vector.reciprocal(out=inv[:], in_=total[:])
 
         def finish(g, p, column, queue):
-            y = keep.tile([P, H], F32, name=f"y{g}", align_bytes=64)
+            y = keep.tile([P, H], F32, name=f"y{column}", align_bytes=64)
             nc.vector.tensor_scalar(out=y[:], in0=p, scalar1=inv[:], scalar2=shift_k[:, g : g + 1], op0=ALU.mult, op1=ALU.mult)
             queue.dma_start(out=out[:, column : column + H], in_=y[:])
 
         finish(0, p_b0[:], I, nc.sync)
         finish(1, p_a[:, 0:H], 0, nc.scalar)
         finish(2, p_a[:, H:I], H, nc.sync)
-        finish(3, p_last[:, 0:H], I + H, nc.scalar)
+        finish(3, p_last[:], I + H, nc.scalar)

@@ -29,7 +29,7 @@ def interleave(copy, grouped, raw):
     )
 
 
-SPLIT0 = 64
+E = 128
 
 
 def tile_attend_contrastprobs_kernel(tc, query, bank_words, bank_scales, bkey, tmp, offs, out):
@@ -49,113 +49,101 @@ def tile_attend_contrastprobs_kernel(tc, query, bank_words, bank_scales, bkey, t
         tmp_col = keep.tile([P, 1], F32, name="tmp_col")
         nc.scalar.dma_start(out=tmp_col[:], in_=tmp)
 
-        k0_raw = keep.tile([P, PACK, H], F32, name="k0_raw", align_bytes=64)
-        nc.sync.dma_start(out=k0_raw[:], in_=keys[:, :, 0:H])
+        q_raw = keep.tile([P, PACK, Q], F32, name="q_raw", align_bytes=64)
+        nc.sync.dma_start(out=q_raw[:], in_=query.rearrange("(p t) q -> p t q", t=PACK))
+        k0_raw = keep.tile([P, PACK, E], F32, name="k0_raw", align_bytes=64)
+        nc.sync.dma_start(out=k0_raw[:], in_=keys[:, :, 0:E])
         offsets = keep.tile([P, I // 16], U16, name="offsets")
         nc.sync.dma_start(offsets[:], offs)
         nc.sync.dma_start(out=spread[ROW0 : ROW0 + 64 : 4, :].bitcast(I32), in_=bank_scales[0].bitcast(I32))
-        q_raw = big.tile([P, PACK, Q], F32, name="q_raw", offset=0)
-        nc.sync.dma_start(out=q_raw[:], in_=query.rearrange("(p t) q -> p t q", t=PACK))
-        words = big.tile([P, T], U16, name="words", offset=4096)
+        words = big.tile([P, T], U16, name="words", offset=0)
         nc.sync.dma_start(out=words[:].bitcast(I32), in_=bank_words[0].bitcast(I32))
-        k1_raw = big.tile([P, PACK, H // 2], F32, name="k1_raw", offset=12288)
-        nc.sync.dma_start(out=k1_raw[:], in_=keys[:, :, H : H + H // 2])
+        k_raw = [k0_raw]
+        for c in range(1, 4):
+            raw = big.tile([P, PACK, E], F32, name=f"k{c}_raw", offset=2 * T + 2048 * c)
+            nc.sync.dma_start(out=raw[:], in_=keys[:, :, c * E : (c + 1) * E])
+            k_raw.append(raw)
 
-        k2_raw = big.tile([P, PACK, H // 2], F32, name="k2_raw", offset=14336)
-        nc.sync.dma_start(out=k2_raw[:], in_=keys[:, :, H + H // 2 : J])
+        def grouped(name, raw, copy):
+            tile = keep.tile([P, E, PACK], BF16, name=name + "_grouped", align_bytes=64)
+            interleave(copy, tile[:], raw[:])
+            return tile
 
-        k0_grouped = keep.tile([P, H, PACK], BF16, name="k0_grouped", align_bytes=64)
-        interleave(nc.vector.tensor_copy, k0_grouped[:, 0:SPLIT0, :], k0_raw[:, :, 0:SPLIT0])
-        interleave(nc.scalar.copy, k0_grouped[:, SPLIT0:H, :], k0_raw[:, :, SPLIT0:H])
+        def quantize(name, tile):
+            codes = keep.tile([P, E], U32, name=name + "_codes", align_bytes=64)
+            scales = keep.tile([P, E], U8, name=name + "_scales", align_bytes=64)
+            nc.vector.quantize_mx(out=codes[:].bitcast(FP8X4), scales=scales[:], in_=tile[:].rearrange("p j t -> p (j t)"))
+            return codes[:].bitcast(FP8X4), scales[:]
+
         neg_tmp = keep.tile([P, 1], F32, name="neg_tmp")
         nc.vector.tensor_scalar(out=neg_tmp[:], in0=tmp_col[:], scalar1=-1.0, scalar2=None, op0=ALU.mult)
-        q_grouped = keep.tile([P, Q, PACK], BF16, name="q_grouped", align_bytes=64)
-        interleave(nc.scalar.copy, q_grouped[:], q_raw[:])
+        q_codes, q_scales = quantize("q", grouped("q", q_raw, nc.scalar.copy))
+        k0_grouped = grouped("k0", k0_raw, nc.scalar.copy)
 
-        picked_scales = keep.tile([P, I], U8, name="picked_scales", tag="k1_scales", align_bytes=64)
+        picked_scales = keep.tile([P, I], U8, name="picked_scales", tag="k2_scales", align_bytes=64)
         nc.vector.tensor_copy(picked_scales[:], spread[:].indirect(offsets[:]))
         for g in range(4):
-            nc.sync.dma_start(out=a_scales[32 * g : 32 * g + 4, :].bitcast(I32), in_=picked_scales[ROW0 + 16 * g : ROW0 + 16 * g + 16 : 4, :].bitcast(I32))
-
-        def quantize(name, grouped, n):
-            codes = keep.tile([P, n], U32, name=name + "_codes", align_bytes=64)
-            scales = keep.tile([P, n], U8, name=name + "_scales", align_bytes=64)
-            nc.vector.quantize_mx(out=codes[:].bitcast(FP8X4), scales=scales[:], in_=grouped[:].rearrange("p j t -> p (j t)"))
-            return codes, scales
-
-        k0_codes, k0_scales = quantize("k0", k0_grouped, H)
-        q_codes, q_scales = quantize("q", q_grouped, Q)
+            nc.scalar.dma_start(out=a_scales[32 * g : 32 * g + 4, :].bitcast(I32), in_=picked_scales[ROW0 + 16 * g : ROW0 + 16 * g + 16 : 4, :].bitcast(I32))
 
         def scores(acc, codes, scales):
-            nc.tensor.matmul_mx(out=acc, lhsT=q_codes[:].bitcast(FP8X4), lhsT_scale=q_scales[:],
-                                rhs=codes, rhs_scale=scales, start=True, stop=True)
+            nc.tensor.matmul_mx(out=acc, lhsT=q_codes, lhsT_scale=q_scales, rhs=codes, rhs_scale=scales, start=True, stop=True)
 
-        b0_sum = psum.tile([Q, H], F32, name="b0_sum")
-        a0_sum = psum.tile([Q, H], F32, name="a0_sum")
-        a1_sum = psum.tile([Q, H], F32, name="a1_sum")
-        b1_sum = psum.tile([Q, H], F32, name="b1_sum")
+        GROUPS = [(I, H), (0, H), (H, H), (I + H, H)]
+        lows = keep.tile([P, len(GROUPS)], F32, name="lows")
+        sums = keep.tile([P, len(GROUPS)], F32, name="sums")
+        banks = [psum.tile([Q, width], F32, name=f"bank{g}") for g, (column, width) in enumerate(GROUPS)]
+        p = keep.tile([P, I + J], F32, name="p", align_bytes=64)
 
-        neg_last = keep.tile([P, H], F32, name="neg_last", align_bytes=64)
-        lows = keep.tile([P, 4], F32, name="lows")
-        sums = keep.tile([P, 8], F32, name="sums")
+        def weigh(g):
+            column, width = GROUPS[g]
+            neg = keep.tile([P, width], F32, name=f"neg{g}", tag="k3_grouped" if g == 0 else f"neg{g}", align_bytes=64)
+            nc.vector.tensor_scalar(out=neg[:], in0=banks[g][:], scalar1=neg_tmp[:], scalar2=None,
+                                    op0=ALU.mult, op1=ALU.min, accum_out=lows[:, g : g + 1])
+            nc.scalar.activation(out=p[:, column : column + width], in_=neg[:], func=ACT.Exp, scale=-1.0,
+                                 bias=lows[:, g : g + 1], accum_out=sums[:, g : g + 1])
 
-        def low(g):
-            return lows[:, g : g + 1]
-
-        def negate(g, acc, neg):
-            nc.vector.tensor_scalar(out=neg, in0=acc, scalar1=neg_tmp[:], scalar2=None,
-                                    op0=ALU.mult, op1=ALU.min, accum_out=low(g))
-
-        def weights(g, neg, p):
-            nc.scalar.activation(out=p, in_=neg, func=ACT.Exp, scale=-1.0, bias=low(g), accum_out=sums[:, g : g + 1])
-
-        scores(b0_sum[:], k0_codes[:].bitcast(FP8X4), k0_scales[:])
-        neg_b0 = keep.tile([P, H], F32, name="neg_b0", align_bytes=64)
-        negate(0, b0_sum[:], neg_b0[:])
-        p_b0 = keep.tile([P, H], F32, name="p_b0", align_bytes=64)
-        weights(0, neg_b0[:], p_b0[:])
+        scores(banks[0][:, 0:E], *quantize("k0", k0_grouped))
 
         picked_words = keep.tile([P, I], U16, name="picked_words", align_bytes=64)
         nc.vector.tensor_copy(picked_words[:], words[:].indirect(offsets[:]))
-        scores(a0_sum[:], picked_words[:, 0:H].bitcast(FP4X4), a_scales[:, 0:H])
-        scores(a1_sum[:], picked_words[:, H:I].bitcast(FP4X4), a_scales[:, H:I])
+        scores(banks[1][:], picked_words[:, 0:H].bitcast(FP4X4), a_scales[:, 0:H])
+        scores(banks[2][:], picked_words[:, H:I].bitcast(FP4X4), a_scales[:, H:I])
 
-        k1_grouped = keep.tile([P, H // 2, PACK], BF16, name="k1_grouped", align_bytes=64)
-        interleave(nc.scalar.copy, k1_grouped[:], k1_raw[:])
-        k1_codes, k1_scales = quantize("k1", k1_grouped, H // 2)
-        k2_grouped = keep.tile([P, H // 2, PACK], BF16, name="k2_grouped", align_bytes=64)
-        interleave(nc.vector.tensor_copy, k2_grouped[:], k2_raw[:])
-
-        neg_a = keep.tile([P, I], F32, name="neg_a", align_bytes=64)
-        p_a = keep.tile([P, I], F32, name="p_a", align_bytes=64)
-        k2_codes, k2_scales = quantize("k2", k2_grouped, H // 2)
-        scores(b1_sum[:, 0 : H // 2], k1_codes[:].bitcast(FP8X4), k1_scales[:])
-        scores(b1_sum[:, H // 2 : H], k2_codes[:].bitcast(FP8X4), k2_scales[:])
-        negate(1, a0_sum[:], neg_a[:, 0:H])
-        weights(1, neg_a[:, 0:H], p_a[:, 0:H])
-        negate(2, a1_sum[:], neg_a[:, H:I])
-        weights(2, neg_a[:, H:I], p_a[:, H:I])
-        negate(3, b1_sum[:], neg_last[:])
-        p_last = keep.tile([P, H], F32, name="p_last", align_bytes=64)
-        weights(3, neg_last[:], p_last[:])
+        k1_grouped = grouped("k1", k_raw[1], nc.scalar.copy)
+        k2_grouped = grouped("k2", k_raw[2], nc.scalar.copy)
+        k1_mx = quantize("k1", k1_grouped)
+        k3_grouped = grouped("k3", k_raw[3], nc.vector.tensor_copy)
+        scores(banks[0][:, E:H], *k1_mx)
+        scores(banks[3][:, 0:E], *quantize("k2", k2_grouped))
+        scores(banks[3][:, E:H], *quantize("k3", k3_grouped))
+        for g in range(len(GROUPS)):
+            weigh(g)
 
         lowest = keep.tile([P, 1], F32, name="lowest")
         nc.vector.tensor_reduce(out=lowest[:], in_=lows[:], axis=mybir.AxisListType.X, op=ALU.min)
-        shift_k = keep.tile([P, 4], F32, name="shift_k")
-        nc.scalar.activation(out=shift_k[:], in_=lows[:], func=ACT.Exp, scale=-1.0, bias=lowest[:])
-        terms = keep.tile([P, 4], F32, name="terms")
+        shifts = keep.tile([P, len(GROUPS)], F32, name="shifts")
+        nc.scalar.activation(out=shifts[:], in_=lows[:], func=ACT.Exp, scale=-1.0, bias=lowest[:])
+        terms = keep.tile([P, len(GROUPS)], F32, name="terms")
         total = keep.tile([P, 1], F32, name="total")
-        nc.vector.scalar_tensor_tensor(out=terms[:], in0=sums[:, 0:4], scalar=1.0 / OUT_SCALE, in1=shift_k[:],
+        nc.vector.scalar_tensor_tensor(out=terms[:], in0=sums[:], scalar=1.0 / OUT_SCALE, in1=shifts[:],
                                        op0=ALU.mult, op1=ALU.mult, accum_out=total[:])
         inv = keep.tile([P, 1], F32, name="inv")
         nc.vector.reciprocal(out=inv[:], in_=total[:])
 
-        def finish(g, p, column, queue):
-            y = keep.tile([P, H], F32, name=f"y{column}", align_bytes=64)
-            nc.vector.tensor_scalar(out=y[:], in0=p, scalar1=inv[:], scalar2=shift_k[:, g : g + 1], op0=ALU.mult, op1=ALU.mult)
-            queue.dma_start(out=out[:, column : column + H], in_=y[:])
+        y = keep.tile([P, I + J], F32, name="y", align_bytes=64)
 
-        finish(0, p_b0[:], I, nc.sync)
-        finish(1, p_a[:, 0:H], 0, nc.scalar)
-        finish(2, p_a[:, H:I], H, nc.sync)
-        finish(3, p_last[:], I + H, nc.scalar)
+        def finish(g):
+            column, width = GROUPS[g]
+            nc.vector.tensor_scalar(out=y[:, column : column + width], in0=p[:, column : column + width], scalar1=inv[:],
+                                    scalar2=shifts[:, g : g + 1], op0=ALU.mult, op1=ALU.mult)
+
+        def store(queue, first, last):
+            queue.dma_start(out=out[:, first:last], in_=y[:, first:last])
+
+        finish(1)
+        store(nc.sync, 0, H)
+        finish(2)
+        finish(0)
+        store(nc.scalar, H, I + H)
+        finish(3)
+        store(nc.sync, I + H, I + J)

@@ -69,10 +69,17 @@ def tile_attend_contrastprobs_kernel(tc, query, bank_words, bank_scales, bkey, t
             interleave(copy, tile[:], raw[:])
             return tile
 
+        def planes(name, width):
+            codes = keep.tile([P, width], U32, name=name + "_codes", align_bytes=64)
+            scales = keep.tile([P, width], U8, name=name + "_scales", align_bytes=64)
+            return codes, scales
+
+        def quantize_into(codes, scales, tile):
+            nc.vector.quantize_mx(out=codes.bitcast(FP8X4), scales=scales, in_=tile[:].rearrange("p j t -> p (j t)"))
+
         def quantize(name, tile):
-            codes = keep.tile([P, E], U32, name=name + "_codes", align_bytes=64)
-            scales = keep.tile([P, E], U8, name=name + "_scales", align_bytes=64)
-            nc.vector.quantize_mx(out=codes[:].bitcast(FP8X4), scales=scales[:], in_=tile[:].rearrange("p j t -> p (j t)"))
+            codes, scales = planes(name, E)
+            quantize_into(codes[:], scales[:], tile)
             return codes[:].bitcast(FP8X4), scales[:]
 
         neg_tmp = keep.tile([P, 1], F32, name="neg_tmp")
@@ -96,7 +103,7 @@ def tile_attend_contrastprobs_kernel(tc, query, bank_words, bank_scales, bkey, t
 
         def weigh(g):
             column, width = GROUPS[g]
-            neg = keep.tile([P, width], F32, name=f"neg{g}", tag="k3_grouped" if g == 0 else f"neg{g}", align_bytes=64)
+            neg = keep.tile([P, width], F32, name=f"neg{g}", tag="k2_grouped" if g == 0 else f"neg{g}", align_bytes=64)
             nc.vector.tensor_scalar(out=neg[:], in0=banks[g][:], scalar1=neg_tmp[:], scalar2=None,
                                     op0=ALU.mult, op1=ALU.min, accum_out=lows[:, g : g + 1])
             nc.scalar.activation(out=p[:, column : column + width], in_=neg[:], func=ACT.Exp, scale=-1.0,
@@ -114,8 +121,10 @@ def tile_attend_contrastprobs_kernel(tc, query, bank_words, bank_scales, bkey, t
         k1_mx = quantize("k1", k1_grouped)
         k3_grouped = grouped("k3", k_raw[3], nc.vector.tensor_copy)
         scores(banks[0][:, E:H], *k1_mx)
-        scores(banks[3][:, 0:E], *quantize("k2", k2_grouped))
-        scores(banks[3][:, E:H], *quantize("k3", k3_grouped))
+        late_codes, late_scales = planes("k2", H)
+        quantize_into(late_codes[:, 0:E], late_scales[:, 0:E], k2_grouped)
+        quantize_into(late_codes[:, E:H], late_scales[:, E:H], k3_grouped)
+        scores(banks[3][:], late_codes[:].bitcast(FP8X4), late_scales[:])
         for g in range(len(GROUPS)):
             weigh(g)
 

@@ -40,38 +40,38 @@ def tile_attend_contrastprobs_kernel(tc, query, bank_words, bank_scales, bkey, t
         psum = ctx.enter_context(tc.psum_pool(name="psum", bufs=1))
         keys = bkey.rearrange("(p t) j -> p t j", t=PACK)
 
-        zeros = big.tile([P, 16384], U8, name="zeros", offset=0)
+        zeros = big.tile([P, 16384], U8, name="zeros", offset=0, align_bytes=256)
         nc.vector.memset(zeros[:, 0:I].bitcast(I32), 0)
-        spread = keep.tile([P, T], U8, name="spread", align_bytes=64)
+        spread = keep.tile([P, T], U8, name="spread", align_bytes=256)
         nc.vector.memset(spread[:].bitcast(I32), 0)
-        a_scales = keep.tile([P, I], U8, name="a_scales", align_bytes=64)
+        a_scales = keep.tile([P, I], U8, name="a_scales", align_bytes=256)
         nc.vector.tensor_copy(out=a_scales[:].bitcast(I32), in_=zeros[:, 0:I].bitcast(I32))
         tmp_col = keep.tile([P, 1], F32, name="tmp_col")
         nc.scalar.dma_start(out=tmp_col[:], in_=tmp)
 
-        q_raw = keep.tile([P, PACK, Q], F32, name="q_raw", align_bytes=64)
+        q_raw = keep.tile([P, PACK, Q], F32, name="q_raw", align_bytes=256)
         nc.sync.dma_start(out=q_raw[:], in_=query.rearrange("(p t) q -> p t q", t=PACK))
-        k0_raw = keep.tile([P, PACK, E], F32, name="k0_raw", align_bytes=64)
+        k0_raw = keep.tile([P, PACK, E], F32, name="k0_raw", align_bytes=256)
         nc.sync.dma_start(out=k0_raw[:], in_=keys[:, :, 0:E])
-        offsets = keep.tile([P, I // 16], U16, name="offsets")
+        offsets = keep.tile([P, I // 16], U16, name="offsets", align_bytes=256)
         nc.sync.dma_start(offsets[:], offs)
         nc.sync.dma_start(out=spread[ROW0 : ROW0 + 64 : 4, :].bitcast(I32), in_=bank_scales[0].bitcast(I32))
-        words = big.tile([P, T], U16, name="words", offset=0)
+        words = big.tile([P, T], U16, name="words", offset=0, align_bytes=256)
         nc.sync.dma_start(out=words[:].bitcast(I32), in_=bank_words[0].bitcast(I32))
         k_raw = [k0_raw]
         for c in range(1, 4):
-            raw = big.tile([P, PACK, E], F32, name=f"k{c}_raw", offset=2 * T + 2048 * c)
+            raw = big.tile([P, PACK, E], F32, name=f"k{c}_raw", offset=2 * T + 2048 * c, align_bytes=256)
             nc.sync.dma_start(out=raw[:], in_=keys[:, :, c * E : (c + 1) * E])
             k_raw.append(raw)
 
         def grouped(name, raw, copy):
-            tile = keep.tile([P, E, PACK], BF16, name=name + "_grouped", align_bytes=64)
+            tile = keep.tile([P, E, PACK], BF16, name=name + "_grouped", align_bytes=256)
             interleave(copy, tile[:], raw[:])
             return tile
 
         def planes(name, width):
-            codes = keep.tile([P, width], U32, name=name + "_codes", align_bytes=64)
-            scales = keep.tile([P, width], U8, name=name + "_scales", align_bytes=64)
+            codes = keep.tile([P, width], U32, name=name + "_codes", align_bytes=256)
+            scales = keep.tile([P, width], U8, name=name + "_scales", align_bytes=256)
             return codes, scales
 
         def quantize_into(codes, scales, tile):
@@ -87,7 +87,7 @@ def tile_attend_contrastprobs_kernel(tc, query, bank_words, bank_scales, bkey, t
         q_codes, q_scales = quantize("q", grouped("q", q_raw, nc.scalar.copy))
         k0_grouped = grouped("k0", k0_raw, nc.scalar.copy)
 
-        picked_scales = keep.tile([P, I], U8, name="picked_scales", tag="k2_scales", align_bytes=64)
+        picked_scales = keep.tile([P, I], U8, name="picked_scales", tag="k2_scales", align_bytes=256)
         nc.vector.tensor_copy(picked_scales[:], spread[:].indirect(offsets[:]))
         for g in range(4):
             nc.scalar.dma_start(out=a_scales[32 * g : 32 * g + 4, :].bitcast(I32), in_=picked_scales[ROW0 + 16 * g : ROW0 + 16 * g + 16 : 4, :].bitcast(I32))
@@ -99,11 +99,11 @@ def tile_attend_contrastprobs_kernel(tc, query, bank_words, bank_scales, bkey, t
         lows = keep.tile([P, len(GROUPS)], F32, name="lows")
         sums = keep.tile([P, len(GROUPS)], F32, name="sums")
         banks = [psum.tile([Q, width], F32, name=f"bank{g}") for g, (column, width) in enumerate(GROUPS)]
-        p = keep.tile([P, I + J], F32, name="p", align_bytes=64)
+        p = keep.tile([P, I + J], F32, name="p", align_bytes=256)
 
         def weigh(g):
             column, width = GROUPS[g]
-            neg = keep.tile([P, width], F32, name=f"neg{g}", tag="k2_grouped" if g == 0 else f"neg{g}", align_bytes=64)
+            neg = keep.tile([P, width], F32, name=f"neg{g}", tag="k2_grouped" if g == 0 else f"neg{g}", align_bytes=256)
             nc.vector.tensor_scalar(out=neg[:], in0=banks[g][:], scalar1=neg_tmp[:], scalar2=None,
                                     op0=ALU.mult, op1=ALU.min, accum_out=lows[:, g : g + 1])
             nc.scalar.activation(out=p[:, column : column + width], in_=neg[:], func=ACT.Exp, scale=-1.0,
@@ -111,7 +111,7 @@ def tile_attend_contrastprobs_kernel(tc, query, bank_words, bank_scales, bkey, t
 
         scores(banks[0][:, 0:E], *quantize("k0", k0_grouped))
 
-        picked_words = keep.tile([P, I], U16, name="picked_words", align_bytes=64)
+        picked_words = keep.tile([P, I], U16, name="picked_words", align_bytes=256)
         nc.vector.tensor_copy(picked_words[:], words[:].indirect(offsets[:]))
         scores(banks[1][:], picked_words[:, 0:H].bitcast(FP4X4), a_scales[:, 0:H])
         scores(banks[2][:], picked_words[:, H:I].bitcast(FP4X4), a_scales[:, H:I])
@@ -139,7 +139,7 @@ def tile_attend_contrastprobs_kernel(tc, query, bank_words, bank_scales, bkey, t
         inv = keep.tile([P, 1], F32, name="inv")
         nc.vector.reciprocal(out=inv[:], in_=total[:])
 
-        y = keep.tile([P, I + J], F32, name="y", align_bytes=64)
+        y = keep.tile([P, I + J], F32, name="y", align_bytes=256)
 
         def finish(g):
             column, width = GROUPS[g]

@@ -95,7 +95,7 @@ def tile_attend_contrastprobs_kernel(tc, query, bank_words, bank_scales, bkey, t
         def scores(acc, codes, scales):
             nc.tensor.matmul_mx(out=acc, lhsT=q_codes, lhsT_scale=q_scales, rhs=codes, rhs_scale=scales, start=True, stop=True)
 
-        GROUPS = [(I, H), (0, H), (H, H), (I + H, H)]
+        GROUPS = [(I, E), (I + E, E), (0, H), (H, H), (I + H, H)]
         lows = keep.tile([P, len(GROUPS)], F32, name="lows")
         sums = keep.tile([P, len(GROUPS)], F32, name="sums")
         banks = [psum.tile([Q, width], F32, name=f"bank{g}") for g, (column, width) in enumerate(GROUPS)]
@@ -103,29 +103,30 @@ def tile_attend_contrastprobs_kernel(tc, query, bank_words, bank_scales, bkey, t
 
         def weigh(g):
             column, width = GROUPS[g]
-            neg = keep.tile([P, width], F32, name=f"neg{g}", tag="k2_grouped" if g == 0 else f"neg{g}", align_bytes=256)
+            neg = keep.tile([P, width], F32, name=f"neg{g}", tag="k2_grouped" if g == 1 else f"neg{g}", align_bytes=256)
             nc.vector.tensor_scalar(out=neg[:], in0=banks[g][:], scalar1=neg_tmp[:], scalar2=None,
                                     op0=ALU.mult, op1=ALU.min, accum_out=lows[:, g : g + 1])
             nc.scalar.activation(out=p[:, column : column + width], in_=neg[:], func=ACT.Exp, scale=-1.0,
                                  bias=lows[:, g : g + 1], accum_out=sums[:, g : g + 1])
 
-        scores(banks[0][:, 0:E], *quantize("k0", k0_grouped))
+        scores(banks[0][:], *quantize("k0", k0_grouped))
+        weigh(0)
 
         picked_words = keep.tile([P, I], U16, name="picked_words", align_bytes=256)
         nc.vector.tensor_copy(picked_words[:], words[:].indirect(offsets[:]))
-        scores(banks[1][:], picked_words[:, 0:H].bitcast(FP4X4), a_scales[:, 0:H])
-        scores(banks[2][:], picked_words[:, H:I].bitcast(FP4X4), a_scales[:, H:I])
+        scores(banks[2][:], picked_words[:, 0:H].bitcast(FP4X4), a_scales[:, 0:H])
+        scores(banks[3][:], picked_words[:, H:I].bitcast(FP4X4), a_scales[:, H:I])
 
         k1_grouped = grouped("k1", k_raw[1], nc.scalar.copy)
         k2_grouped = grouped("k2", k_raw[2], nc.scalar.copy)
         k1_mx = quantize("k1", k1_grouped)
         k3_grouped = grouped("k3", k_raw[3], nc.vector.tensor_copy)
-        scores(banks[0][:, E:H], *k1_mx)
+        scores(banks[1][:], *k1_mx)
         late_codes, late_scales = planes("k2", H)
         quantize_into(late_codes[:, 0:E], late_scales[:, 0:E], k2_grouped)
         quantize_into(late_codes[:, E:H], late_scales[:, E:H], k3_grouped)
-        scores(banks[3][:], late_codes[:].bitcast(FP8X4), late_scales[:])
-        for g in range(len(GROUPS)):
+        scores(banks[4][:], late_codes[:].bitcast(FP8X4), late_scales[:])
+        for g in range(1, len(GROUPS)):
             weigh(g)
 
         lowest = keep.tile([P, 1], F32, name="lowest")
@@ -149,10 +150,11 @@ def tile_attend_contrastprobs_kernel(tc, query, bank_words, bank_scales, bkey, t
         def store(queue, first, last):
             queue.dma_start(out=out[:, first:last], in_=y[:, first:last])
 
-        finish(1)
-        store(nc.sync, 0, H)
         finish(2)
-        finish(0)
-        store(nc.scalar, H, I + H)
+        store(nc.sync, 0, H)
         finish(3)
+        finish(0)
+        finish(1)
+        store(nc.scalar, H, I + H)
+        finish(4)
         store(nc.sync, I + H, I + J)

@@ -18,6 +18,8 @@ PACK = 4
 D, T, I, J, Q = 512, 4096, 512, 512, 128
 H = 256
 ROW0 = 32
+Z = 32
+CLEAR = 3072
 OUT_SCALE = 1024.0
 FLOPS = 2 * D * Q * (I + J)
 
@@ -41,11 +43,13 @@ def tile_attend_contrastprobs_kernel(tc, query, bank_words, bank_scales, bkey, t
         keys = bkey.rearrange("(p t) j -> p t j", t=PACK)
 
         zeros = big.tile([P, 16384], U8, name="zeros", offset=0, align_bytes=256)
-        nc.vector.memset(zeros[:, 0:I].bitcast(I32), 0)
+        nc.vector.memset(zeros[:, 0:Z].bitcast(I32), 0)
         spread = keep.tile([P, T], U8, name="spread", align_bytes=256)
-        nc.vector.memset(spread[:].bitcast(I32), 0)
+        nc.vector.memset(spread[:, 0:CLEAR].bitcast(I32), 0)
+        nc.gpsimd.memset(spread[:, CLEAR:T].bitcast(I32), 0)
         a_scales = keep.tile([P, I], U8, name="a_scales", align_bytes=256)
-        nc.vector.tensor_copy(out=a_scales[:].bitcast(I32), in_=zeros[:, 0:I].bitcast(I32))
+        nc.vector.tensor_copy(out=a_scales[:, 0:Z].bitcast(I32), in_=zeros[:, 0:Z].bitcast(I32))
+        nc.vector.memset(a_scales[:, Z:I].bitcast(I32), 0)
         tmp_col = keep.tile([P, 1], F32, name="tmp_col")
         nc.scalar.dma_start(out=tmp_col[:], in_=tmp)
 

@@ -19,6 +19,7 @@ D, T, I, J, Q = 512, 4096, 512, 512, 128
 H = 256
 ROW0 = 32
 Z = 32
+SHARE = 88
 CLEAR = 3072
 OUT_SCALE = 1024.0
 FLOPS = 2 * D * Q * (I + J)
@@ -60,13 +61,18 @@ def tile_attend_contrastprobs_kernel(tc, query, bank_words, bank_scales, bkey, t
         offsets = keep.tile([P, I // 16], U16, name="offsets", align_bytes=256)
         nc.sync.dma_start(offsets[:], offs)
         nc.sync.dma_start(out=spread[ROW0 : ROW0 + 64 : 4, :].bitcast(I32), in_=bank_scales[0].bitcast(I32))
-        words = big.tile([P, T], U16, name="words", offset=0, align_bytes=256)
-        nc.sync.dma_start(out=words[:].bitcast(I32), in_=bank_words[0].bitcast(I32))
         k_raw = [k0_raw]
-        for c in range(1, 4):
+
+        def load_keys(c):
             raw = big.tile([P, PACK, E], F32, name=f"k{c}_raw", offset=2 * T + 2048 * c, align_bytes=256)
             nc.sync.dma_start(out=raw[:], in_=keys[:, :, c * E : (c + 1) * E])
             k_raw.append(raw)
+
+        load_keys(1)
+        words = big.tile([P, T], U16, name="words", offset=0, align_bytes=256)
+        nc.sync.dma_start(out=words[:].bitcast(I32), in_=bank_words[0].bitcast(I32))
+        load_keys(2)
+        load_keys(3)
 
         def grouped(name, raw, copy):
             tile = keep.tile([P, E, PACK], BF16, name=name + "_grouped", align_bytes=256)
@@ -94,12 +100,12 @@ def tile_attend_contrastprobs_kernel(tc, query, bank_words, bank_scales, bkey, t
         picked_scales = keep.tile([P, I], U8, name="picked_scales", tag="k2_scales", align_bytes=256)
         nc.vector.tensor_copy(picked_scales[:], spread[:].indirect(offsets[:]))
         for g in range(4):
-            nc.scalar.dma_start(out=a_scales[32 * g : 32 * g + 4, :].bitcast(I32), in_=picked_scales[ROW0 + 16 * g : ROW0 + 16 * g + 16 : 4, :].bitcast(I32))
+            nc.sync.dma_start(out=a_scales[32 * g : 32 * g + 4, :].bitcast(I32), in_=picked_scales[ROW0 + 16 * g : ROW0 + 16 * g + 16 : 4, :].bitcast(I32))
 
         def scores(acc, codes, scales):
             nc.tensor.matmul_mx(out=acc, lhsT=q_codes, lhsT_scale=q_scales, rhs=codes, rhs_scale=scales, start=True, stop=True)
 
-        GROUPS = [(I, E), (I + E, E), (0, H), (H, H), (I + H, H)]
+        GROUPS = [(I, H), (0, H), (H, H), (I + H, H)]
         lows = keep.tile([P, len(GROUPS)], F32, name="lows")
         sums = keep.tile([P, len(GROUPS)], F32, name="sums")
         banks = [psum.tile([Q, width], F32, name=f"bank{g}") for g, (column, width) in enumerate(GROUPS)]
@@ -113,23 +119,25 @@ def tile_attend_contrastprobs_kernel(tc, query, bank_words, bank_scales, bkey, t
             nc.scalar.activation(out=p[:, column : column + width], in_=neg[:], func=ACT.Exp, scale=-1.0,
                                  bias=lows[:, g : g + 1], accum_out=sums[:, g : g + 1])
 
-        scores(banks[0][:], *quantize("k0", k0_grouped))
+        early_codes, early_scales = planes("k0", H)
+        quantize_into(early_codes[:, 0:E], early_scales[:, 0:E], k0_grouped)
+        quantize_into(early_codes[:, E:H], early_scales[:, E:H], grouped("k1", k_raw[1], nc.scalar.copy))
+        scores(banks[0][:], early_codes[:].bitcast(FP8X4), early_scales[:])
         weigh(0)
 
         picked_words = keep.tile([P, I], U16, name="picked_words", align_bytes=256)
         nc.vector.tensor_copy(picked_words[:], words[:].indirect(offsets[:]))
-        scores(banks[2][:], picked_words[:, 0:H].bitcast(FP4X4), a_scales[:, 0:H])
-        scores(banks[3][:], picked_words[:, H:I].bitcast(FP4X4), a_scales[:, H:I])
+        scores(banks[1][:], picked_words[:, 0:H].bitcast(FP4X4), a_scales[:, 0:H])
+        scores(banks[2][:], picked_words[:, H:I].bitcast(FP4X4), a_scales[:, H:I])
 
-        k1_grouped = grouped("k1", k_raw[1], nc.scalar.copy)
         k2_grouped = grouped("k2", k_raw[2], nc.scalar.copy)
-        k1_mx = quantize("k1", k1_grouped)
-        k3_grouped = grouped("k3", k_raw[3], nc.vector.tensor_copy)
-        scores(banks[1][:], *k1_mx)
+        k3_grouped = keep.tile([P, E, PACK], BF16, name="k3_grouped", align_bytes=256)
+        interleave(nc.vector.tensor_copy, k3_grouped[:, 0:SHARE, :], k_raw[3][:, :, 0:SHARE])
+        interleave(nc.scalar.copy, k3_grouped[:, SHARE:E, :], k_raw[3][:, :, SHARE:E])
         late_codes, late_scales = planes("k2", H)
         quantize_into(late_codes[:, 0:E], late_scales[:, 0:E], k2_grouped)
         quantize_into(late_codes[:, E:H], late_scales[:, E:H], k3_grouped)
-        scores(banks[4][:], late_codes[:].bitcast(FP8X4), late_scales[:])
+        scores(banks[3][:], late_codes[:].bitcast(FP8X4), late_scales[:])
         for g in range(1, len(GROUPS)):
             weigh(g)
 
@@ -154,11 +162,10 @@ def tile_attend_contrastprobs_kernel(tc, query, bank_words, bank_scales, bkey, t
         def store(queue, first, last):
             queue.dma_start(out=out[:, first:last], in_=y[:, first:last])
 
-        finish(2)
-        store(nc.sync, 0, H)
-        finish(3)
-        finish(0)
         finish(1)
+        store(nc.sync, 0, H)
+        finish(2)
+        finish(0)
         store(nc.scalar, H, I + H)
-        finish(4)
+        finish(3)
         store(nc.sync, I + H, I + J)

@@ -20,6 +20,7 @@ H = 256
 ROW0 = 32
 Z = 32
 SHARE = 88
+EARLY_SHARE = 160
 CLEAR = 3072
 OUT_SCALE = 1024.0
 FLOPS = 2 * D * Q * (I + J)
@@ -54,29 +55,23 @@ def tile_attend_contrastprobs_kernel(tc, query, bank_words, bank_scales, bkey, t
         tmp_col = keep.tile([P, 1], F32, name="tmp_col")
         nc.scalar.dma_start(out=tmp_col[:], in_=tmp)
 
-        q_raw = keep.tile([P, PACK, Q], F32, name="q_raw", align_bytes=256)
-        nc.sync.dma_start(out=q_raw[:], in_=query.rearrange("(p t) q -> p t q", t=PACK))
-        k0_raw = keep.tile([P, PACK, E], F32, name="k0_raw", align_bytes=256)
-        nc.sync.dma_start(out=k0_raw[:], in_=keys[:, :, 0:E])
+        early_raw = keep.tile([P, PACK, H], F32, name="early_raw", align_bytes=256)
+        nc.sync.dma_start(out=early_raw[:], in_=keys[:, :, 0:H])
         offsets = keep.tile([P, I // 16], U16, name="offsets", align_bytes=256)
         nc.sync.dma_start(offsets[:], offs)
         nc.sync.dma_start(out=spread[ROW0 : ROW0 + 64 : 4, :].bitcast(I32), in_=bank_scales[0].bitcast(I32))
-        k_raw = [k0_raw]
-
-        def load_keys(c):
-            raw = big.tile([P, PACK, E], F32, name=f"k{c}_raw", offset=2 * T + 2048 * c, align_bytes=256)
-            nc.sync.dma_start(out=raw[:], in_=keys[:, :, c * E : (c + 1) * E])
-            k_raw.append(raw)
-
-        load_keys(1)
+        q_raw = big.tile([P, PACK, Q], F32, name="q_raw", offset=2 * T, align_bytes=256)
+        nc.sync.dma_start(out=q_raw[:], in_=query.rearrange("(p t) q -> p t q", t=PACK))
         words = big.tile([P, T], U16, name="words", offset=0, align_bytes=256)
         nc.sync.dma_start(out=words[:].bitcast(I32), in_=bank_words[0].bitcast(I32))
-        load_keys(2)
-        load_keys(3)
+        k_raw = {}
+        for c in (2, 3):
+            k_raw[c] = big.tile([P, PACK, E], F32, name=f"k{c}_raw", offset=2 * T + 2048 * c, align_bytes=256)
+            nc.sync.dma_start(out=k_raw[c][:], in_=keys[:, :, c * E : (c + 1) * E])
 
         def grouped(name, raw, copy):
             tile = keep.tile([P, E, PACK], BF16, name=name + "_grouped", align_bytes=256)
-            interleave(copy, tile[:], raw[:])
+            interleave(copy, tile[:], raw)
             return tile
 
         def planes(name, width):
@@ -94,8 +89,9 @@ def tile_attend_contrastprobs_kernel(tc, query, bank_words, bank_scales, bkey, t
 
         neg_tmp = keep.tile([P, 1], F32, name="neg_tmp")
         nc.vector.tensor_scalar(out=neg_tmp[:], in0=tmp_col[:], scalar1=-1.0, scalar2=None, op0=ALU.mult)
-        q_codes, q_scales = quantize("q", grouped("q", q_raw, nc.scalar.copy))
-        k0_grouped = grouped("k0", k0_raw, nc.scalar.copy)
+        early_grouped = keep.tile([P, H, PACK], BF16, name="early_grouped", align_bytes=256)
+        interleave(nc.scalar.copy, early_grouped[:, 0:EARLY_SHARE, :], early_raw[:, :, 0:EARLY_SHARE])
+        interleave(nc.vector.tensor_copy, early_grouped[:, EARLY_SHARE:H, :], early_raw[:, :, EARLY_SHARE:H])
 
         picked_scales = keep.tile([P, I], U8, name="picked_scales", tag="k2_scales", align_bytes=256)
         nc.vector.tensor_copy(picked_scales[:], spread[:].indirect(offsets[:]))
@@ -119,9 +115,10 @@ def tile_attend_contrastprobs_kernel(tc, query, bank_words, bank_scales, bkey, t
             nc.scalar.activation(out=p[:, column : column + width], in_=neg[:], func=ACT.Exp, scale=-1.0,
                                  bias=lows[:, g : g + 1], accum_out=sums[:, g : g + 1])
 
+        q_grouped = grouped("q", q_raw[:], nc.scalar.copy)
         early_codes, early_scales = planes("k0", H)
-        quantize_into(early_codes[:, 0:E], early_scales[:, 0:E], k0_grouped)
-        quantize_into(early_codes[:, E:H], early_scales[:, E:H], grouped("k1", k_raw[1], nc.scalar.copy))
+        quantize_into(early_codes[:], early_scales[:], early_grouped)
+        q_codes, q_scales = quantize("q", q_grouped)
         scores(banks[0][:], early_codes[:].bitcast(FP8X4), early_scales[:])
         weigh(0)
 
@@ -130,7 +127,7 @@ def tile_attend_contrastprobs_kernel(tc, query, bank_words, bank_scales, bkey, t
         scores(banks[1][:], picked_words[:, 0:H].bitcast(FP4X4), a_scales[:, 0:H])
         scores(banks[2][:], picked_words[:, H:I].bitcast(FP4X4), a_scales[:, H:I])
 
-        k2_grouped = grouped("k2", k_raw[2], nc.scalar.copy)
+        k2_grouped = grouped("k2", k_raw[2][:], nc.scalar.copy)
         k3_grouped = keep.tile([P, E, PACK], BF16, name="k3_grouped", align_bytes=256)
         interleave(nc.vector.tensor_copy, k3_grouped[:, 0:SHARE, :], k_raw[3][:, :, 0:SHARE])
         interleave(nc.scalar.copy, k3_grouped[:, SHARE:E, :], k_raw[3][:, :, SHARE:E])

from contextlib import ExitStack

import concourse.mybir as mybir

F32 = mybir.dt.float32
BF16 = mybir.dt.bfloat16
I32 = mybir.dt.int32
U32 = mybir.dt.uint32
U16 = mybir.dt.uint16
U8 = mybir.dt.uint8
FP8X4 = mybir.dt.float8_e4m3fn_x4
FP4X4 = mybir.dt.float4_e2m1fn_x4
ALU = mybir.AluOpType
ACT = mybir.ActivationFunctionType

P = 128
PACK = 4
D, T, I, J, Q = 512, 4096, 512, 512, 128
H = 256
ROW0 = 32
Z = 32
SHARE = 88
EARLY_SHARE = 160
CLEAR = 3072
OUT_SCALE = 1024.0
FLOPS = 2 * D * Q * (I + J)


def interleave(copy, grouped, raw):
    copy(
        out=grouped.rearrange("p (c i) t -> p c t i", i=4),
        in_=raw.rearrange("p t (c i) -> p c t i", i=4),
    )


E = 128


def tile_attend_contrastprobs_kernel(tc, query, bank_words, bank_scales, bkey, tmp, offs, out):
    nc = tc.nc
    with ExitStack() as ctx:
        keep = ctx.enter_context(tc.tile_pool(name="keep", bufs=1))
        big = ctx.enter_context(tc.tile_pool(name="big", bufs=1))
        psum = ctx.enter_context(tc.psum_pool(name="psum", bufs=1))
        keys = bkey.rearrange("(p t) j -> p t j", t=PACK)

        zeros = big.tile([P, 16384], U8, name="zeros", offset=0, align_bytes=256)
        nc.vector.memset(zeros[:, 0:Z].bitcast(I32), 0)
        spread = keep.tile([P, T], U8, name="spread", align_bytes=256)
        nc.vector.memset(spread[:, 0:CLEAR].bitcast(I32), 0)
        nc.gpsimd.memset(spread[:, CLEAR:T].bitcast(I32), 0)
        a_scales = keep.tile([P, I], U8, name="a_scales", align_bytes=256)
        nc.vector.tensor_copy(out=a_scales[:, 0:Z].bitcast(I32), in_=zeros[:, 0:Z].bitcast(I32))
        nc.vector.memset(a_scales[:, Z:I].bitcast(I32), 0)
        tmp_col = keep.tile([P, 1], F32, name="tmp_col")
        nc.scalar.dma_start(out=tmp_col[:], in_=tmp)

        early_raw = keep.tile([P, PACK, H], F32, name="early_raw", align_bytes=256)
        nc.sync.dma_start(out=early_raw[:], in_=keys[:, :, 0:H])
        offsets = keep.tile([P, I // 16], U16, name="offsets", align_bytes=256)
        nc.sync.dma_start(offsets[:], offs)
        nc.sync.dma_start(out=spread[ROW0 : ROW0 + 64 : 4, :].bitcast(I32), in_=bank_scales[0].bitcast(I32))
        q_raw = big.tile([P, PACK, Q], F32, name="q_raw", offset=2 * T, align_bytes=256)
        nc.sync.dma_start(out=q_raw[:], in_=query.rearrange("(p t) q -> p t q", t=PACK))
        words = big.tile([P, T], U16, name="words", offset=0, align_bytes=256)
        nc.sync.dma_start(out=words[:].bitcast(I32), in_=bank_words[0].bitcast(I32))
        k_raw = {}
        for c in (2, 3):
            k_raw[c] = big.tile([P, PACK, E], F32, name=f"k{c}_raw", offset=2 * T + 2048 * c, align_bytes=256)
            nc.sync.dma_start(out=k_raw[c][:], in_=keys[:, :, c * E : (c + 1) * E])

        def grouped(name, raw, copy):
            tile = keep.tile([P, E, PACK], BF16, name=name + "_grouped", align_bytes=256)
            interleave(copy, tile[:], raw)
            return tile

        def planes(name, width):
            codes = keep.tile([P, width], U32, name=name + "_codes", align_bytes=256)
            scales = keep.tile([P, width], U8, name=name + "_scales", align_bytes=256)
            return codes, scales

        def quantize_into(codes, scales, tile):
            nc.vector.quantize_mx(out=codes.bitcast(FP8X4), scales=scales, in_=tile[:].rearrange("p j t -> p (j t)"))

        def quantize(name, tile):
            codes, scales = planes(name, E)
            quantize_into(codes[:], scales[:], tile)
            return codes[:].bitcast(FP8X4), scales[:]

        neg_tmp = keep.tile([P, 1], F32, name="neg_tmp")
        nc.vector.tensor_scalar(out=neg_tmp[:], in0=tmp_col[:], scalar1=-1.0, scalar2=None, op0=ALU.mult)
        early_grouped = keep.tile([P, H, PACK], BF16, name="early_grouped", align_bytes=256)
        interleave(nc.scalar.copy, early_grouped[:, 0:EARLY_SHARE, :], early_raw[:, :, 0:EARLY_SHARE])
        interleave(nc.vector.tensor_copy, early_grouped[:, EARLY_SHARE:H, :], early_raw[:, :, EARLY_SHARE:H])

        picked_scales = keep.tile([P, I], U8, name="picked_scales", tag="k2_scales", align_bytes=256)
        nc.vector.tensor_copy(picked_scales[:], spread[:].indirect(offsets[:]))
        for g in range(4):
            nc.sync.dma_start(out=a_scales[32 * g : 32 * g + 4, :].bitcast(I32), in_=picked_scales[ROW0 + 16 * g : ROW0 + 16 * g + 16 : 4, :].bitcast(I32))

        def scores(acc, codes, scales):
            nc.tensor.matmul_mx(out=acc, lhsT=q_codes, lhsT_scale=q_scales, rhs=codes, rhs_scale=scales, start=True, stop=True)

        GROUPS = [(I, H), (0, H), (H, H), (I + H, H)]
        lows = keep.tile([P, len(GROUPS)], F32, name="lows")
        sums = keep.tile([P, len(GROUPS)], F32, name="sums")
        banks = [psum.tile([Q, width], F32, name=f"bank{g}") for g, (column, width) in enumerate(GROUPS)]
        p = keep.tile([P, I + J], F32, name="p", align_bytes=256)

        def weigh(g):
            column, width = GROUPS[g]
            neg = keep.tile([P, width], F32, name=f"neg{g}", tag="k2_grouped" if g == 1 else f"neg{g}", align_bytes=256)
            nc.vector.tensor_scalar(out=neg[:], in0=banks[g][:], scalar1=neg_tmp[:], scalar2=None,
                                    op0=ALU.mult, op1=ALU.min, accum_out=lows[:, g : g + 1])
            nc.scalar.activation(out=p[:, column : column + width], in_=neg[:], func=ACT.Exp, scale=-1.0,
                                 bias=lows[:, g : g + 1], accum_out=sums[:, g : g + 1])

        q_grouped = grouped("q", q_raw[:], nc.scalar.copy)
        early_codes, early_scales = planes("k0", H)
        quantize_into(early_codes[:], early_scales[:], early_grouped)
        q_codes, q_scales = quantize("q", q_grouped)
        scores(banks[0][:], early_codes[:].bitcast(FP8X4), early_scales[:])
        weigh(0)

        picked_words = keep.tile([P, I], U16, name="picked_words", align_bytes=256)
        nc.vector.tensor_copy(picked_words[:], words[:].indirect(offsets[:]))
        scores(banks[1][:], picked_words[:, 0:H].bitcast(FP4X4), a_scales[:, 0:H])
        scores(banks[2][:], picked_words[:, H:I].bitcast(FP4X4), a_scales[:, H:I])

        k2_grouped = grouped("k2", k_raw[2][:], nc.scalar.copy)
        k3_grouped = keep.tile([P, E, PACK], BF16, name="k3_grouped", align_bytes=256)
        interleave(nc.vector.tensor_copy, k3_grouped[:, 0:SHARE, :], k_raw[3][:, :, 0:SHARE])
        interleave(nc.scalar.copy, k3_grouped[:, SHARE:E, :], k_raw[3][:, :, SHARE:E])
        late_codes, late_scales = planes("k2", H)
        quantize_into(late_codes[:, 0:E], late_scales[:, 0:E], k2_grouped)
        quantize_into(late_codes[:, E:H], late_scales[:, E:H], k3_grouped)
        scores(banks[3][:], late_codes[:].bitcast(FP8X4), late_scales[:])
        for g in range(1, len(GROUPS)):
            weigh(g)

        lowest = keep.tile([P, 1], F32, name="lowest")
        nc.vector.tensor_reduce(out=lowest[:], in_=lows[:], axis=mybir.AxisListType.X, op=ALU.min)
        shifts = keep.tile([P, len(GROUPS)], F32, name="shifts")
        nc.scalar.activation(out=shifts[:], in_=lows[:], func=ACT.Exp, scale=-1.0, bias=lowest[:])
        terms = keep.tile([P, len(GROUPS)], F32, name="terms")
        total = keep.tile([P, 1], F32, name="total")
        nc.vector.scalar_tensor_tensor(out=terms[:], in0=sums[:], scalar=1.0 / OUT_SCALE, in1=shifts[:],
                                       op0=ALU.mult, op1=ALU.mult, accum_out=total[:])
        inv = keep.tile([P, 1], F32, name="inv")
        nc.vector.reciprocal(out=inv[:], in_=total[:])

        y = keep.tile([P, I + J], F32, name="y", align_bytes=256)

        def finish(g):
            column, width = GROUPS[g]
            nc.vector.tensor_scalar(out=y[:, column : column + width], in0=p[:, column : column + width], scalar1=inv[:],
                                    scalar2=shifts[:, g : g + 1], op0=ALU.mult, op1=ALU.mult)

        def store(queue, first, last):
            queue.dma_start(out=out[:, first:last], in_=y[:, first:last])

        finish(1)
        store(nc.sync, 0, H)
        finish(2)
        finish(0)
        store(nc.scalar, H, I + H)
        finish(3)
        store(nc.sync, I + H, I + J)
